import numpy as np
import ml_dtypes


def mxq(x, axis, fmt="e4m3"):
    dtype, down = {"e4m3": (ml_dtypes.float8_e4m3fn, 7), "e5m2": (ml_dtypes.float8_e5m2, 14)}[fmt]
    v = np.moveaxis(np.asarray(x, np.float32).astype(ml_dtypes.bfloat16).astype(np.float64), axis, -1)
    blocks = v.reshape(v.shape[:-1] + (-1, 32))
    amax = np.abs(blocks).max(-1, keepdims=True)
    byte = np.maximum(np.where(amax > 0, np.frexp(amax)[1] - 1 + 127, 0) - down, 1)
    scale = np.exp2(byte - 127.0)
    codes = (blocks / scale).astype(np.float32).astype(dtype).astype(np.float64)
    return np.moveaxis((codes * scale).reshape(v.shape), -1, axis)


WIDE = False


def mx_kscale(k):
    if not WIDE:
        return np.ones(k)
    levels = np.array([10, -10, 5, -5, 0])
    if k % 512:
        return np.exp2(np.random.permutation(np.resize(levels, k // 32))).repeat(32)
    a = np.empty((k // 512, 16))
    for p in range(k // 512):
        a[p, :8] = np.random.permutation(np.resize(levels, 8))
        for g in range(8):
            far = levels[np.abs(levels - a[p, g]) >= 10]
            a[p, g + 8] = far[np.random.randint(len(far))]
    return np.exp2(a.ravel()).repeat(32)


def f64(x):
    return np.asarray(x).astype(np.float64)


def striped(idx):
    return np.tile(idx.reshape(-1, 16).T, (8, 1)).astype(np.uint16)


def unstriped(offs):
    return offs[:16].T.reshape(-1).astype(np.int64)


E2M1 = np.array([0.0, 0.5, 1.0, 1.5, 2.0, 3.0, 4.0, 6.0, -0.0, -0.5, -1.0, -1.5, -2.0, -3.0, -4.0, -6.0])


def pack_weight(w, fmt):
    k, n = w.shape
    w = f64(np.asarray(w, np.float32).astype(ml_dtypes.bfloat16)).reshape(k // 32, 32, n)
    amax = np.abs(w).max(1)
    if fmt == "e4m3":
        byte = np.frexp(amax)[1] - 1 + 127 - 7
    else:
        mant, ex = np.frexp(amax / 6.0)
        byte = np.where(mant > 0.5, ex, ex - 1) + 127
    byte = np.clip(np.where(amax > 0, byte, 1), 1, 254)
    scaled = (w * np.exp2(127.0 - byte)[:, None, :]).reshape(k, n).astype(np.float32)
    by_word = np.ascontiguousarray(scaled.reshape(k // 512, 128, 4, n).transpose(0, 1, 3, 2))
    if fmt == "e4m3":
        words = by_word.astype(ml_dtypes.float8_e4m3fn).view(np.uint8)
    else:
        c = by_word.astype(ml_dtypes.float4_e2m1fn).view(np.uint8) & 0xF
        words = (c[..., 0::2] | (c[..., 1::2] << 4)).reshape(k // 512, 128, 2 * n)
    return np.ascontiguousarray(words), np.ascontiguousarray(byte.astype(np.uint8).reshape(k // 512, 16, n))


def unpack_weight(words, scales, fmt):
    g, _, n = scales.shape
    words = np.ascontiguousarray(words).reshape(g, 128, n, -1)
    if fmt == "e4m3":
        vals = words.view(ml_dtypes.float8_e4m3fn).astype(np.float64)
    else:
        nib = np.empty((g, 128, n, 4), np.uint8)
        nib[..., 0::2] = words & 0xF
        nib[..., 1::2] = words >> 4
        vals = E2M1[nib]
    vals = vals * np.repeat(np.exp2(scales.astype(np.float64) - 127.0), 8, axis=1)[..., None]
    return vals.transpose(0, 1, 3, 2).reshape(g * 512, n)


def gelu(v):
    return 0.5 * v * (1.0 + np.tanh(np.sqrt(2.0 / np.pi) * (v + 0.044715 * v**3)))


K, T, S, H, N = 1024, 4096, 1024, 1024, 512


def setup_inputs():
    n = np.random.standard_normal
    s = mx_kscale(K)[:, None]
    u = mx_kscale(H)[:, None]
    tab_words, tab_scales = pack_weight(n((K, T)) * s, "e2m1")
    w2_words, w2_scales = pack_weight(n((K, H)) / np.sqrt(K) / s, "e4m3")
    w3_words, w3_scales = pack_weight(n((H, N)) / np.sqrt(H) / u, "e2m1")
    return {
        "tab_words": tab_words, "tab_scales": tab_scales,
        "offs": striped(np.random.permutation(T)[:S]),
        "offs2": striped(np.random.permutation(T)[:S]),
        "w1": (n((K, H)) / np.sqrt(K) / s * u.T).astype(np.float32),
        "w2_words": w2_words, "w2_scales": w2_scales,
        "low": (0.7 * n(H) * u[:, 0]).astype(np.float32),
        "high": (0.6 * n(H) * u[:, 0]).astype(np.float32),
        "w3_words": w3_words, "w3_scales": w3_scales,
        "bias": (0.5 * n(N)).astype(np.float32),
    }


def reference(tab_words, tab_scales, offs, offs2, w1, w2_words, w2_scales,
              low, high, w3_words, w3_scales, bias):
    TW = unpack_weight(tab_words, tab_scales, "e2m1")
    v = TW[:, unstriped(offs)]
    v2 = TW[:, unstriped(offs2)]
    a = mxq(f64(w1), 0, "e4m3").T @ v
    b = unpack_weight(w2_words, w2_scales, "e4m3").T @ v2
    h = (f64(high)[:, None] * b + a) * b + f64(low)[:, None]
    hq = mxq(h, 0, "e4m3")
    y = unpack_weight(w3_words, w3_scales, "e2m1").T @ hq
    return y + f64(bias)[:, None]

@@ -1,0 +1,268 @@
+from contextlib import ExitStack
+
+import concourse.mybir as mybir
+
+K, T, S, H, N = 1024, 4096, 1024, 1024, 512
+FLOPS = 2 * (2 * K * H * S + H * N * S)
+
+F32 = mybir.dt.float32
+BF16 = mybir.dt.bfloat16
+I32 = mybir.dt.int32
+U32 = mybir.dt.uint32
+U16 = mybir.dt.uint16
+U8 = mybir.dt.uint8
+FP8X4 = mybir.dt.float8_e4m3fn_x4
+FP4X4 = mybir.dt.float4_e2m1fn_x4
+MULT = mybir.AluOpType.mult
+ADD = mybir.AluOpType.add
+IDENT = mybir.ActivationFunctionType.Identity
+
+P = 128
+PACK = 4
+KP = P * PACK
+W = 512
+WEAVE = "scalar"
+
+
+def tile_list_pavement_upstream_horner_kernel(
+    tc, tab_words, tab_scales, offs, offs2, w1, w2_words, w2_scales, low, high, w3_words, w3_scales, bias, out
+):
+    nc = tc.nc
+    with ExitStack() as ctx:
+        keep = ctx.enter_context(tc.tile_pool(name="keep", bufs=1))
+        ring = ctx.enter_context(tc.tile_pool(name="ring", bufs=3))
+        psum = ctx.enter_context(tc.psum_pool(name="psum", bufs=1))
+
+        def held(name, shape, dtype):
+            return keep.tile(shape, dtype, name=name, align_bytes=64)
+
+        lists = [held("list_a", [P, S // 16], U16), held("list_b", [P, S // 16], U16)]
+        nc.sync.dma_start(lists[0][:], offs)
+        nc.sync.dma_start(lists[1][:], offs2)
+
+        tab_s = held("tab_s", [P, T], U8)
+        nc.vector.memset(tab_s[:].bitcast(I32), 0)
+        w2s_raw = held("w2s_raw", [P, 2, H], U8)
+        nc.gpsimd.memset(w2s_raw[:].rearrange("p a c -> p (a c)").bitcast(I32), 0)
+        vs1 = held("vs1", [P, 2 * S], U8)
+        nc.vector.memset(vs1[:].bitcast(I32), 0)
+        w3s = held("w3s", [P, 2, N], U8)
+        nc.vector.memset(w3s[:].rearrange("p a c -> p (a c)").bitcast(I32), 0)
+
+        for q in range(4):
+            nc.sync.dma_start(tab_s[32 * q : 32 * q + 8, :].bitcast(I32), tab_scales[:, 4 * q : 4 * q + 4, :].bitcast(I32))
+        for q in range(4):
+            nc.gpsimd.dma_start(
+                w2s_raw[32 * q : 32 * q + 4, :, :].bitcast(I32),
+                w2_scales[:, 4 * q : 4 * q + 4, :].rearrange("a r c -> r a c").bitcast(I32),
+            )
+        high_t = held("high_t", [P, 2, PACK], F32)
+        low_t = held("low_t", [P, 2, PACK], F32)
+        nc.gpsimd.dma_start(high_t[:], high.rearrange("(g p t) -> p g t", g=2, t=PACK))
+        nc.gpsimd.dma_start(low_t[:], low.rearrange("(g p t) -> p g t", g=2, t=PACK))
+
+        tab_w = [held("tab_w%d" % a, [P, T], U16) for a in range(2)]
+        w1_raw = {}
+        w2_raw = {}
+
+        def load_tab(a):
+            nc.sync.dma_start(tab_w[a][:].bitcast(I32), tab_words[a].bitcast(I32))
+
+        def load_w1(g, a):
+            w1_raw[g, a] = held("w1_raw%d%d" % (g, a), [P, PACK, KP], F32)
+            rows = w1[KP * a : KP * (a + 1), KP * g : KP * (g + 1)]
+            nc.sync.dma_start(w1_raw[g, a][:], rows.rearrange("(p j) c -> p j c", j=PACK))
+
+        def load_w2(g):
+            w2_raw[g] = held("w2_raw%d" % g, [P, 2, KP], U32)
+            words = w2_words.rearrange("a p c i -> p a (c i)")[:, :, PACK * KP * g : PACK * KP * (g + 1)]
+            nc.sync.dma_start(w2_raw[g][:].bitcast(I32), words.bitcast(I32))
+
+        load_tab(0)
+        load_w1(0, 0)
+        load_w1(0, 1)
+        load_tab(1)
+        load_w2(0)
+
+        vs0 = held("vs0", [P, 2 * S], U8)
+        for l in range(2):
+            nc.vector.tensor_copy(vs0[:, S * l : S * (l + 1)], tab_s[:].indirect(lists[l][:]))
+        for q in range(4):
+            nc.sync.dma_start(vs1[32 * q : 32 * q + 4, :].bitcast(I32), vs0[32 * q + 4 : 32 * q + 8, :].bitcast(I32))
+        v_s = [vs0, vs1]
+
+        load_w1(1, 0)
+        load_w1(1, 1)
+        load_w2(1)
+        w3w = held("w3w", [P, 2, N], U16)
+        nc.sync.dma_start(w3w[:].bitcast(I32), w3_words.rearrange("a p b -> p a b").bitcast(I32))
+        for q in range(4):
+            nc.sync.dma_start(
+                w3s[32 * q : 32 * q + 4, :, :].bitcast(I32),
+                w3_scales[:, 4 * q : 4 * q + 4, :].rearrange("a r c -> r a c").bitcast(I32),
+            )
+        bias_t = held("bias_t", [P, N // P], F32)
+        with nc.allow_non_contiguous_dma("bias: one value a partition"):
+            nc.sync.dma_start(bias_t[:], bias.rearrange("(c p) -> p c", p=P))
+
+        v_w = {}
+
+        def gather_words(l, a, s):
+            v_w[l, a, s] = held("v_w%d%d%d" % (l, a, s), [P, W], U16)
+            cols = slice(W // 16 * s, W // 16 * (s + 1))
+            nc.vector.tensor_copy(v_w[l, a, s][:], tab_w[a][:].indirect(lists[l][:, cols]))
+
+        w1_bf, w1_c, w1_s, w2_c, w2_s = {}, {}, {}, {}, {}
+
+        def cast_w1(g, a):
+            w1_bf[g, a] = held("w1_bf%d%d" % (g, a), [P, PACK * KP], BF16)
+            nc.scalar.copy(
+                w1_bf[g, a][:].rearrange("p (t m j) -> p m j t", t=PACK, j=PACK),
+                w1_raw[g, a][:].rearrange("p j (m t) -> p m j t", t=PACK),
+            )
+
+        def quant_w1(g, a):
+            w1_c[g, a] = held("w1_c%d%d" % (g, a), [P, KP], U32)
+            w1_s[g, a] = held("w1_s%d%d" % (g, a), [P, KP], U8)
+            nc.vector.quantize_mx(out=w1_c[g, a][:].bitcast(FP8X4), scales=w1_s[g, a][:], in_=w1_bf[g, a][:])
+
+        def order_w2(g):
+            w2_c[g] = held("w2_c%d" % g, [P, 2, KP], U32)
+            w2_s[g] = held("w2_s%d" % g, [P, 2, KP], U8)
+            nc.vector.tensor_copy(
+                w2_s[g][:].rearrange("p a (t m) -> p a m t", t=PACK),
+                w2s_raw[:, :, KP * g : KP * (g + 1)].rearrange("p a (m t) -> p a m t", t=PACK),
+            )
+            nc.vector.tensor_copy(
+                w2_c[g][:].bitcast(I32).rearrange("p a (t m) -> p a m t", t=PACK),
+                w2_raw[g][:].bitcast(I32).rearrange("p a (m t) -> p a m t", t=PACK),
+            )
+
+        cast_w1(0, 0)
+        cast_w1(0, 1)
+        for s in range(2):
+            for l in range(2):
+                gather_words(l, 0, s)
+        quant_w1(0, 0)
+        gather_words(0, 1, 0)
+        quant_w1(0, 1)
+        gather_words(1, 1, 0)
+        order_w2(0)
+
+        def bank(i):
+            return psum.tile([P, W], F32, name="bank%d" % i, tag="bank%d" % i)
+
+        units = [(0, 0), (0, 1), (1, 0), (1, 1)]
+        steps = [(g, s, t) for g, s in units for t in range(PACK)]
+        a_sb, b_ps, inner, prod, planes, woven, h_c, h_s = {}, {}, {}, {}, {}, {}, {}, {}
+
+        def products(i):
+            g, s, t = steps[i]
+            cols = slice(P * t, P * (t + 1))
+            a_ps = bank(i % 2)
+            for a in range(2):
+                nc.tensor.matmul_mx(
+                    out=a_ps[:], lhsT=w1_c[g, a][:, cols].bitcast(FP8X4), lhsT_scale=w1_s[g, a][:, cols],
+                    rhs=v_w[0, a, s][:].bitcast(FP4X4), rhs_scale=v_s[a][:, W * s : W * (s + 1)],
+                    start=(a == 0), stop=(a == 1))
+            b_ps[i] = bank(2 + i % 4)
+            for a in range(2):
+                nc.tensor.matmul_mx(
+                    out=b_ps[i][:], lhsT=w2_c[g][:, a, cols].bitcast(FP8X4), lhsT_scale=w2_s[g][:, a, cols],
+                    rhs=v_w[1, a, s][:].bitcast(FP4X4), rhs_scale=v_s[a][:, S + W * s : S + W * (s + 1)],
+                    start=(a == 0), stop=(a == 1))
+            a_sb[i] = ring.tile([P, W], F32, name="a_sb", tag="a_sb")
+            nc.scalar.copy(a_sb[i][:], a_ps[:])
+
+        def horner1(i):
+            g, s, t = steps[i]
+            inner[i] = ring.tile([P, W], F32, name="inner", tag="inner")
+            nc.vector.scalar_tensor_tensor(inner[i][:], b_ps[i][:], high_t[:, g, t : t + 1], a_sb[i][:], MULT, ADD)
+
+        def horner2(i):
+            g, s, t = steps[i]
+            prod[i] = ring.tile([P, W], F32, name="prod", tag="prod")
+            nc.vector.tensor_tensor(prod[i][:], b_ps[i][:], inner[i][:], MULT)
+            if t == 0:
+                planes[g, s] = ring.tile([P, PACK, W], BF16, name="planes", tag="planes")
+            if i < n - 2:
+                nc.gpsimd.tensor_scalar(planes[g, s][:, t, :], prod[i][:], 1.0, low_t[:, g, t : t + 1], MULT, ADD)
+            else:
+                nc.scalar.activation(planes[g, s][:, t, :], prod[i][:], IDENT, bias=low_t[:, g, t : t + 1])
+
+        def weave(g, s, part, eng):
+            if part == 0:
+                woven[g, s] = held("woven%d%d" % (g, s), [P, W, PACK], BF16)
+            cols = slice(W // 2 * part, W // 2 * (part + 1))
+            dst = woven[g, s][:, cols, :].rearrange("p (c i) t -> p c t i", i=4)
+            src = planes[g, s][:, :, cols].rearrange("p t (c i) -> p c t i", i=4)
+            if eng == "gpsimd":
+                nc.gpsimd.tensor_scalar(dst, src, 1.0, 0.0, MULT, ADD)
+            elif eng == "scalar":
+                nc.scalar.copy(dst, src)
+            else:
+                nc.vector.tensor_copy(dst, src)
+
+        def quant_h(g, s, part):
+            if part == 0:
+                h_c[g, s] = held("h_c%d%d" % (g, s), [P, W], U32)
+                h_s[g, s] = held("h_s%d%d" % (g, s), [P, W], U8)
+            cols = slice(W // 2 * part, W // 2 * (part + 1))
+            nc.vector.quantize_mx(out=h_c[g, s][:, cols].bitcast(FP8X4), scales=h_s[g, s][:, cols],
+                                  in_=woven[g, s][:, cols, :].rearrange("p c t -> p (c t)"))
+
+        y_ps = {}
+
+        def mix(s, c, g, b):
+            if g == 0:
+                y_ps[s, c] = bank(b)
+            cols = slice(P * c, P * (c + 1))
+            nc.tensor.matmul_mx(
+                out=y_ps[s, c][:], lhsT=w3w[:, g, cols].bitcast(FP4X4), lhsT_scale=w3s[:, g, cols],
+                rhs=h_c[g, s][:].bitcast(FP8X4), rhs_scale=h_s[g, s][:], start=(g == 0), stop=(g == 1))
+
+        def finish(s, c, eng):
+            res = held("res%d%d" % (s, c), [P, W], F32)
+            if eng == "scalar":
+                nc.scalar.activation(res[:], y_ps[s, c][:], IDENT, bias=bias_t[:, c : c + 1])
+            else:
+                nc.vector.tensor_scalar_add(res[:], y_ps[s, c][:], bias_t[:, c : c + 1])
+            nc.sync.dma_start(out[P * c : P * (c + 1), W * s : W * (s + 1)], res[:])
+
+        extras = {
+            1: [lambda: gather_words(0, 1, 1), lambda: cast_w1(1, 0)],
+            2: [lambda: gather_words(1, 1, 1)],
+            4: [lambda: cast_w1(1, 1), lambda: quant_w1(1, 0)],
+            5: [lambda: order_w2(1)],
+            6: [lambda: quant_w1(1, 1)],
+        }
+        n = len(steps)
+        products(0)
+        products(1)
+        horner1(0)
+        for i in range(n):
+            for f in extras.get(i, []):
+                f()
+            if i + 2 < n:
+                products(i + 2)
+            if i + 1 < n:
+                horner1(i + 1)
+            horner2(i)
+            if i >= 4 and i % 4 == 0:
+                for part in range(2):
+                    weave(*units[i // 4 - 1], part, WEAVE)
+            if i >= 4 and i % 4 in (2, 3):
+                quant_h(*units[i // 4 - 1], i % 4 - 2)
+        for c in range(4):
+            for g in range(2):
+                mix(0, c, g, 6 + c % 2)
+            finish(0, c, "scalar")
+        for c in range(4):
+            mix(1, c, 0, c)
+        weave(1, 1, 0, "vector")
+        weave(1, 1, 1, "vector")
+        quant_h(1, 1, 0)
+        quant_h(1, 1, 1)
+        for c in range(4):
+            mix(1, c, 1, c)
+            finish(1, c, "scalar" if c % 2 == 0 else "vector")

@@ -19,9 +19,18 @@ IDENT = mybir.ActivationFunctionType.Identity
 
 P = 128
 PACK = 4
-KP = P * PACK
-W = 512
-WEAVE = "scalar"
+PASS = P * PACK
+HALF = 512
+PART = 128
+QUADS = 4
+OUT_TILES = N // P
+AHEAD = 3
+RING = 4
+CAST_PARTS = 4
+UNITS = [(0, 0), (0, 1), (1, 0)]
+STEPS = [(g, s, t) for g, s in UNITS for t in range(PACK)]
+LAST_UNIT = len(STEPS) - PACK
+MIX_BANKS = (2, 7)
 
 
 def tile_list_pavement_upstream_horner_kernel(
@@ -30,239 +39,306 @@ def tile_list_pavement_upstream_horner_kernel(
     nc = tc.nc
     with ExitStack() as ctx:
         keep = ctx.enter_context(tc.tile_pool(name="keep", bufs=1))
-        ring = ctx.enter_context(tc.tile_pool(name="ring", bufs=3))
+        ring = ctx.enter_context(tc.tile_pool(name="ring", bufs=RING))
         psum = ctx.enter_context(tc.psum_pool(name="psum", bufs=1))
 
-        def held(name, shape, dtype):
-            return keep.tile(shape, dtype, name=name, align_bytes=64)
+        def held(name, shape, dtype, tag=None):
+            return keep.tile(shape, dtype, name=name, tag=tag or name, align_bytes=64)
+
+        def bank(index, shape):
+            return psum.tile(shape, F32, name="bank", tag="bank%d" % index)
+
+        def load_scale_rows(tile, scales):
+            for q in range(QUADS):
+                rows = scales[:, 4 * q : 4 * q + 4, :].rearrange("a r c -> r a c")
+                nc.sync.dma_start(tile[32 * q : 32 * q + 4, :, :].bitcast(I32), rows.bitcast(I32))
 
         lists = [held("list_a", [P, S // 16], U16), held("list_b", [P, S // 16], U16)]
         nc.sync.dma_start(lists[0][:], offs)
         nc.sync.dma_start(lists[1][:], offs2)
 
         tab_s = held("tab_s", [P, T], U8)
-        nc.vector.memset(tab_s[:].bitcast(I32), 0)
-        w2s_raw = held("w2s_raw", [P, 2, H], U8)
-        nc.gpsimd.memset(w2s_raw[:].rearrange("p a c -> p (a c)").bitcast(I32), 0)
-        vs1 = held("vs1", [P, 2 * S], U8)
-        nc.vector.memset(vs1[:].bitcast(I32), 0)
-        w3s = held("w3s", [P, 2, N], U8)
-        nc.vector.memset(w3s[:].rearrange("p a c -> p (a c)").bitcast(I32), 0)
+        nc.sync.dma_start(tab_s[0:32, :].bitcast(I32), tab_scales.rearrange("a q t -> (a q) t").bitcast(I32))
+        nc.vector.memset(tab_s[32:64, :].bitcast(I32), 0)
+        nc.vector.memset(tab_s[64:128, :].bitcast(I32), 0)
+        w2_s_raw = held("w2_s_raw", [P, 2, H], U8, tag="weight_scales")
+        nc.vector.memset(w2_s_raw[:].rearrange("p a c -> p (a c)").bitcast(I32), 0)
+        v_s_all = held("v_s_all", [P, 4 * S], U8)
+        nc.gpsimd.memset(v_s_all[:].bitcast(I32), 0)
+        v_s = [v_s_all[:, 2 * S * a : 2 * S * (a + 1)] for a in range(2)]
 
-        for q in range(4):
-            nc.sync.dma_start(tab_s[32 * q : 32 * q + 8, :].bitcast(I32), tab_scales[:, 4 * q : 4 * q + 4, :].bitcast(I32))
-        for q in range(4):
-            nc.gpsimd.dma_start(
-                w2s_raw[32 * q : 32 * q + 4, :, :].bitcast(I32),
-                w2_scales[:, 4 * q : 4 * q + 4, :].rearrange("a r c -> r a c").bitcast(I32),
-            )
         high_t = held("high_t", [P, 2, PACK], F32)
         low_t = held("low_t", [P, 2, PACK], F32)
-        nc.gpsimd.dma_start(high_t[:], high.rearrange("(g p t) -> p g t", g=2, t=PACK))
-        nc.gpsimd.dma_start(low_t[:], low.rearrange("(g p t) -> p g t", g=2, t=PACK))
+        nc.sync.dma_start(high_t[:], high.rearrange("(g p t) -> p g t", g=2, t=PACK))
+        nc.sync.dma_start(low_t[:], low.rearrange("(g p t) -> p g t", g=2, t=PACK))
 
         tab_w = [held("tab_w%d" % a, [P, T], U16) for a in range(2)]
-        w1_raw = {}
-        w2_raw = {}
+        w1_raw, w2_raw = {}, {}
 
         def load_tab(a):
             nc.sync.dma_start(tab_w[a][:].bitcast(I32), tab_words[a].bitcast(I32))
 
         def load_w1(g, a):
-            w1_raw[g, a] = held("w1_raw%d%d" % (g, a), [P, PACK, KP], F32)
-            rows = w1[KP * a : KP * (a + 1), KP * g : KP * (g + 1)]
-            nc.sync.dma_start(w1_raw[g, a][:], rows.rearrange("(p j) c -> p j c", j=PACK))
+            w1_raw[g, a] = held("w1_raw", [P, PACK, PASS], F32, tag="w1_raw%d" % a)
+            rows = w1[PASS * a : PASS * (a + 1), PASS * g : PASS * (g + 1)]
+            nc.sync.dma_start(w1_raw[g, a][:], rows.rearrange("(p i) c -> p i c", i=PACK))
 
         def load_w2(g):
-            w2_raw[g] = held("w2_raw%d" % g, [P, 2, KP], U32)
-            words = w2_words.rearrange("a p c i -> p a (c i)")[:, :, PACK * KP * g : PACK * KP * (g + 1)]
+            w2_raw[g] = keep.tile([P, 2, PASS], U32, name="w2_raw", tag="w2_raw")
+            words = w2_words.rearrange("a p c i -> p a (c i)")[:, :, PACK * PASS * g : PACK * PASS * (g + 1)]
             nc.sync.dma_start(w2_raw[g][:].bitcast(I32), words.bitcast(I32))
 
         load_tab(0)
         load_w1(0, 0)
-        load_w1(0, 1)
         load_tab(1)
+        load_scale_rows(w2_s_raw, w2_scales)
+        load_w1(0, 1)
         load_w2(0)
 
-        vs0 = held("vs0", [P, 2 * S], U8)
-        for l in range(2):
-            nc.vector.tensor_copy(vs0[:, S * l : S * (l + 1)], tab_s[:].indirect(lists[l][:]))
-        for q in range(4):
-            nc.sync.dma_start(vs1[32 * q : 32 * q + 4, :].bitcast(I32), vs0[32 * q + 4 : 32 * q + 8, :].bitcast(I32))
-        v_s = [vs0, vs1]
-
-        load_w1(1, 0)
-        load_w1(1, 1)
-        load_w2(1)
-        w3w = held("w3w", [P, 2, N], U16)
-        nc.sync.dma_start(w3w[:].bitcast(I32), w3_words.rearrange("a p b -> p a b").bitcast(I32))
-        for q in range(4):
-            nc.sync.dma_start(
-                w3s[32 * q : 32 * q + 4, :, :].bitcast(I32),
-                w3_scales[:, 4 * q : 4 * q + 4, :].rearrange("a r c -> r a c").bitcast(I32),
-            )
-        bias_t = held("bias_t", [P, N // P], F32)
-        with nc.allow_non_contiguous_dma("bias: one value a partition"):
-            nc.sync.dma_start(bias_t[:], bias.rearrange("(c p) -> p c", p=P))
+        picked_s = held("picked_s", [P, 2 * S], U8)
+        for which in range(2):
+            nc.vector.tensor_copy(picked_s[:, S * which : S * (which + 1)], tab_s[:].indirect(lists[which][:]))
+        for a in range(2):
+            for q in range(QUADS):
+                row = 16 * a + 4 * q
+                nc.sync.dma_start(v_s[a][32 * q : 32 * q + 4, :].bitcast(I32), picked_s[row : row + 4, :].bitcast(I32))
 
         v_w = {}
 
-        def gather_words(l, a, s):
-            v_w[l, a, s] = held("v_w%d%d%d" % (l, a, s), [P, W], U16)
-            cols = slice(W // 16 * s, W // 16 * (s + 1))
-            nc.vector.tensor_copy(v_w[l, a, s][:], tab_w[a][:].indirect(lists[l][:, cols]))
+        def gather_words(which, a, s, room):
+            v_w[which, a, s] = room
+            entries = slice(HALF // 16 * s, HALF // 16 * (s + 1))
+            nc.vector.tensor_copy(room, tab_w[a][:].indirect(lists[which][:, entries]))
+
+        def own_room(which, a, s):
+            return held("v_w%d%d%d" % (which, a, s), [P, HALF], U16)[:]
 
         w1_bf, w1_c, w1_s, w2_c, w2_s = {}, {}, {}, {}, {}
 
-        def cast_w1(g, a):
-            w1_bf[g, a] = held("w1_bf%d%d" % (g, a), [P, PACK * KP], BF16)
-            nc.scalar.copy(
-                w1_bf[g, a][:].rearrange("p (t m j) -> p m j t", t=PACK, j=PACK),
-                w1_raw[g, a][:].rearrange("p j (m t) -> p m j t", t=PACK),
-            )
+        def round_w1(g, a, parts):
+            w1_bf[g, a] = held("w1_bf", [P, PACK * PASS], BF16, tag="w1_bf%d%d" % (g, a))
+            dst = w1_bf[g, a][:].rearrange("p (t m i) -> p m i t", t=PACK, i=PACK)
+            src = w1_raw[g, a][:].rearrange("p i (m t) -> p m i t", t=PACK)
+            for part in range(parts):
+                ms = slice(P // parts * part, P // parts * (part + 1))
+                nc.scalar.copy(dst[:, ms, :, :], src[:, ms, :, :])
 
-        def quant_w1(g, a):
-            w1_c[g, a] = held("w1_c%d%d" % (g, a), [P, KP], U32)
-            w1_s[g, a] = held("w1_s%d%d" % (g, a), [P, KP], U8)
+        def quantise_w1(g, a):
+            w1_c[g, a] = held("w1_c%d%d" % (g, a), [P, PASS], U32)
+            w1_s[g, a] = held("w1_s%d%d" % (g, a), [P, PASS], U8)
             nc.vector.quantize_mx(out=w1_c[g, a][:].bitcast(FP8X4), scales=w1_s[g, a][:], in_=w1_bf[g, a][:])
 
         def order_w2(g):
-            w2_c[g] = held("w2_c%d" % g, [P, 2, KP], U32)
-            w2_s[g] = held("w2_s%d" % g, [P, 2, KP], U8)
+            w2_c[g] = held("w2_c%d" % g, [P, 2, PASS], U32)
+            w2_s[g] = held("w2_s%d" % g, [P, 2, PASS], U8)
             nc.vector.tensor_copy(
                 w2_s[g][:].rearrange("p a (t m) -> p a m t", t=PACK),
-                w2s_raw[:, :, KP * g : KP * (g + 1)].rearrange("p a (m t) -> p a m t", t=PACK),
+                w2_s_raw[:, :, PASS * g : PASS * (g + 1)].rearrange("p a (m t) -> p a m t", t=PACK),
             )
             nc.vector.tensor_copy(
                 w2_c[g][:].bitcast(I32).rearrange("p a (t m) -> p a m t", t=PACK),
                 w2_raw[g][:].bitcast(I32).rearrange("p a (m t) -> p a m t", t=PACK),
             )
 
-        cast_w1(0, 0)
-        cast_w1(0, 1)
+        round_w1(0, 0, 1)
+        round_w1(0, 1, 1)
         for s in range(2):
-            for l in range(2):
-                gather_words(l, 0, s)
-        quant_w1(0, 0)
-        gather_words(0, 1, 0)
-        quant_w1(0, 1)
-        gather_words(1, 1, 0)
+            for which in range(2):
+                gather_words(which, 0, s, own_room(which, 0, s))
+        for which in (1, 0):
+            gather_words(which, 1, 0, own_room(which, 1, 0))
+        quantise_w1(0, 0)
         order_w2(0)
+        quantise_w1(0, 1)
+        load_w1(1, 0)
+        load_w1(1, 1)
+        load_w2(1)
+        late = held("late", [P, 2, HALF], U16, tag="w1_bf01")
+        for which in range(2):
+            gather_words(which, 1, 1, late[:, which, :])
 
-        def bank(i):
-            return psum.tile([P, W], F32, name="bank%d" % i, tag="bank%d" % i)
+        def load_w3():
+            words = held("w3_w", [P, 2, N], U16, tag="w1_raw0")
+            scales = held("w3_s", [P, 2, N], U8, tag="weight_scales")
+            nc.gpsimd.memset(scales[:].rearrange("p a c -> p (a c)").bitcast(I32), 0)
+            nc.sync.dma_start(words[:].bitcast(I32), w3_words.rearrange("a p b -> p a b").bitcast(I32))
+            load_scale_rows(scales, w3_scales)
+            per_row = held("bias_t", [P, OUT_TILES], F32, tag="w1_raw1")
+            with nc.allow_non_contiguous_dma("the bias has one value for each partition of an output tile"):
+                nc.sync.dma_start(per_row[:], bias.rearrange("(c p) -> p c", p=P))
+            return words, scales, per_row
 
-        units = [(0, 0), (0, 1), (1, 0), (1, 1)]
-        steps = [(g, s, t) for g, s in units for t in range(PACK)]
-        a_sb, b_ps, inner, prod, planes, woven, h_c, h_s = {}, {}, {}, {}, {}, {}, {}, {}
-
-        def products(i):
-            g, s, t = steps[i]
+        def product_a(acc, g, s, t, tokens):
             cols = slice(P * t, P * (t + 1))
-            a_ps = bank(i % 2)
             for a in range(2):
                 nc.tensor.matmul_mx(
-                    out=a_ps[:], lhsT=w1_c[g, a][:, cols].bitcast(FP8X4), lhsT_scale=w1_s[g, a][:, cols],
-                    rhs=v_w[0, a, s][:].bitcast(FP4X4), rhs_scale=v_s[a][:, W * s : W * (s + 1)],
-                    start=(a == 0), stop=(a == 1))
-            b_ps[i] = bank(2 + i % 4)
+                    out=acc, lhsT=w1_c[g, a][:, cols].bitcast(FP8X4), lhsT_scale=w1_s[g, a][:, cols],
+                    rhs=v_w[0, a, s][:, tokens].bitcast(FP4X4), rhs_scale=v_s[a][:, HALF * s : HALF * (s + 1)][:, tokens],
+                    start=(a == 0), stop=(a == 1),
+                )
+
+        def product_b(acc, g, s, t, tokens):
+            cols = slice(P * t, P * (t + 1))
             for a in range(2):
                 nc.tensor.matmul_mx(
-                    out=b_ps[i][:], lhsT=w2_c[g][:, a, cols].bitcast(FP8X4), lhsT_scale=w2_s[g][:, a, cols],
-                    rhs=v_w[1, a, s][:].bitcast(FP4X4), rhs_scale=v_s[a][:, S + W * s : S + W * (s + 1)],
-                    start=(a == 0), stop=(a == 1))
-            a_sb[i] = ring.tile([P, W], F32, name="a_sb", tag="a_sb")
-            nc.scalar.copy(a_sb[i][:], a_ps[:])
+                    out=acc, lhsT=w2_c[g][:, a, cols].bitcast(FP8X4), lhsT_scale=w2_s[g][:, a, cols],
+                    rhs=v_w[1, a, s][:, tokens].bitcast(FP4X4),
+                    rhs_scale=v_s[a][:, S + HALF * s : S + HALF * (s + 1)][:, tokens],
+                    start=(a == 0), stop=(a == 1),
+                )
 
-        def horner1(i):
-            g, s, t = steps[i]
-            inner[i] = ring.tile([P, W], F32, name="inner", tag="inner")
-            nc.vector.scalar_tensor_tensor(inner[i][:], b_ps[i][:], high_t[:, g, t : t + 1], a_sb[i][:], MULT, ADD)
-
-        def horner2(i):
-            g, s, t = steps[i]
-            prod[i] = ring.tile([P, W], F32, name="prod", tag="prod")
-            nc.vector.tensor_tensor(prod[i][:], b_ps[i][:], inner[i][:], MULT)
-            if t == 0:
-                planes[g, s] = ring.tile([P, PACK, W], BF16, name="planes", tag="planes")
-            if i < n - 2:
-                nc.gpsimd.tensor_scalar(planes[g, s][:, t, :], prod[i][:], 1.0, low_t[:, g, t : t + 1], MULT, ADD)
-            else:
-                nc.scalar.activation(planes[g, s][:, t, :], prod[i][:], IDENT, bias=low_t[:, g, t : t + 1])
-
-        def weave(g, s, part, eng):
-            if part == 0:
-                woven[g, s] = held("woven%d%d" % (g, s), [P, W, PACK], BF16)
-            cols = slice(W // 2 * part, W // 2 * (part + 1))
-            dst = woven[g, s][:, cols, :].rearrange("p (c i) t -> p c t i", i=4)
-            src = planes[g, s][:, :, cols].rearrange("p t (c i) -> p c t i", i=4)
-            if eng == "gpsimd":
-                nc.gpsimd.tensor_scalar(dst, src, 1.0, 0.0, MULT, ADD)
-            elif eng == "scalar":
-                nc.scalar.copy(dst, src)
-            else:
-                nc.vector.tensor_copy(dst, src)
-
-        def quant_h(g, s, part):
-            if part == 0:
-                h_c[g, s] = held("h_c%d%d" % (g, s), [P, W], U32)
-                h_s[g, s] = held("h_s%d%d" % (g, s), [P, W], U8)
-            cols = slice(W // 2 * part, W // 2 * (part + 1))
-            nc.vector.quantize_mx(out=h_c[g, s][:, cols].bitcast(FP8X4), scales=h_s[g, s][:, cols],
-                                  in_=woven[g, s][:, cols, :].rearrange("p c t -> p (c t)"))
-
-        y_ps = {}
-
-        def mix(s, c, g, b):
-            if g == 0:
-                y_ps[s, c] = bank(b)
+        def product_out(acc, g, c, codes, scales, start, stop):
             cols = slice(P * c, P * (c + 1))
             nc.tensor.matmul_mx(
-                out=y_ps[s, c][:], lhsT=w3w[:, g, cols].bitcast(FP4X4), lhsT_scale=w3s[:, g, cols],
-                rhs=h_c[g, s][:].bitcast(FP8X4), rhs_scale=h_s[g, s][:], start=(g == 0), stop=(g == 1))
+                out=acc, lhsT=w3_w[:, g, cols].bitcast(FP4X4), lhsT_scale=w3_s[:, g, cols],
+                rhs=codes.bitcast(FP8X4), rhs_scale=scales, start=start, stop=stop,
+            )
 
-        def finish(s, c, eng):
-            res = held("res%d%d" % (s, c), [P, W], F32)
-            if eng == "scalar":
-                nc.scalar.activation(res[:], y_ps[s, c][:], IDENT, bias=bias_t[:, c : c + 1])
-            else:
-                nc.vector.tensor_scalar_add(res[:], y_ps[s, c][:], bias_t[:, c : c + 1])
-            nc.sync.dma_start(out[P * c : P * (c + 1), W * s : W * (s + 1)], res[:])
+        addend, b_bank, inner, slices, woven, h_c, h_s = {}, {}, {}, {}, {}, {}, {}
 
-        extras = {
-            1: [lambda: gather_words(0, 1, 1), lambda: cast_w1(1, 0)],
-            2: [lambda: gather_words(1, 1, 1)],
-            4: [lambda: cast_w1(1, 1), lambda: quant_w1(1, 0)],
-            5: [lambda: order_w2(1)],
-            6: [lambda: quant_w1(1, 1)],
-        }
-        n = len(steps)
-        products(0)
-        products(1)
-        horner1(0)
-        for i in range(n):
-            for f in extras.get(i, []):
-                f()
-            if i + 2 < n:
-                products(i + 2)
-            if i + 1 < n:
-                horner1(i + 1)
-            horner2(i)
-            if i >= 4 and i % 4 == 0:
-                for part in range(2):
-                    weave(*units[i // 4 - 1], part, WEAVE)
-            if i >= 4 and i % 4 in (2, 3):
-                quant_h(*units[i // 4 - 1], i % 4 - 2)
-        for c in range(4):
+        def step_products(i):
+            g, s, t = STEPS[i]
+            a_bank = bank(i % 3 if i < LAST_UNIT else i % 2, [P, HALF])
+            product_a(a_bank[:], g, s, t, slice(0, HALF))
+            b_bank[i] = bank(3 + (i % 5 if i < LAST_UNIT else i % 4), [P, HALF])
+            product_b(b_bank[i][:], g, s, t, slice(0, HALF))
+            addend[i] = ring.tile([P, HALF], F32, name="addend", tag="addend")
+            nc.scalar.copy(addend[i][:], a_bank[:])
+
+        def step_inner(i):
+            g, s, t = STEPS[i]
+            inner[i] = ring.tile([P, HALF], F32, name="inner", tag="inner")
+            nc.vector.scalar_tensor_tensor(inner[i][:], b_bank[i][:], high_t[:, g, t : t + 1], addend[i][:], MULT, ADD)
+
+        def step_outer(i):
+            g, s, t = STEPS[i]
+            outer = ring.tile([P, HALF], F32, name="outer", tag="outer")
+            nc.vector.tensor_tensor(outer[:], b_bank[i][:], inner[i][:], MULT)
+            if t == 0:
+                slices[g, s] = ring.tile([P, PACK, HALF], BF16, name="slices", tag="slices")
+            nc.gpsimd.tensor_scalar(slices[g, s][:, t, :], outer[:], 1.0, low_t[:, g, t : t + 1], MULT, ADD)
+
+        def interleave(g, s, piece):
+            if piece == 0:
+                woven[g, s] = held("woven%d%d" % (g, s), [P, HALF, PACK], BF16)
+            tokens = slice(HALF // 2 * piece, HALF // 2 * (piece + 1))
+            nc.scalar.copy(
+                woven[g, s][:, tokens, :].rearrange("p (c e) t -> p c t e", e=4),
+                slices[g, s][:, :, tokens].rearrange("p t (c e) -> p c t e", e=4),
+            )
+
+        def quantise_h(g, s, piece):
+            if piece == 0:
+                h_c[g, s] = held("h_c%d%d" % (g, s), [P, HALF], U32)
+                h_s[g, s] = held("h_s%d%d" % (g, s), [P, HALF], U8)
+            tokens = slice(HALF // 2 * piece, HALF // 2 * (piece + 1))
+            nc.vector.quantize_mx(
+                out=h_c[g, s][:, tokens].bitcast(FP8X4), scales=h_s[g, s][:, tokens],
+                in_=woven[g, s][:, tokens, :].rearrange("p c t -> p (c t)"),
+            )
+
+        def first_half_out(c):
+            acc = bank(MIX_BANKS[c % 2], [P, HALF])
             for g in range(2):
-                mix(0, c, g, 6 + c % 2)
-            finish(0, c, "scalar")
-        for c in range(4):
-            mix(1, c, 0, c)
-        weave(1, 1, 0, "vector")
-        weave(1, 1, 1, "vector")
-        quant_h(1, 1, 0)
-        quant_h(1, 1, 1)
-        for c in range(4):
-            mix(1, c, 1, c)
-            finish(1, c, "scalar" if c % 2 == 0 else "vector")
+                product_out(acc[:], g, c, h_c[g, 0][:], h_s[g, 0][:], g == 0, g == 1)
+            res = held("res%d" % c, [P, HALF], F32)
+            nc.scalar.activation(res[:], acc[:], IDENT, bias=bias_t[:, c : c + 1])
+            nc.sync.dma_start(out[P * c : P * (c + 1), 0:HALF], res[:])
+
+        parts = HALF // PART
+        part_a, part_b, part_scaled, part_inner, part_woven = {}, {}, {}, {}, {}
+
+        def part_products(j):
+            tokens = slice(PART * j, PART * (j + 1))
+            part_a[j] = bank(j % 2, [P, PACK, PART])
+            part_b[j] = bank(3 + j, [P, PACK, PART])
+            for t in range(PACK):
+                product_b(part_b[j][:, t, :], 1, 1, t, tokens)
+            for t in range(PACK):
+                product_a(part_a[j][:, t, :], 1, 1, t, tokens)
+            part_scaled[j] = ring.tile([P, PACK, PART], F32, name="addend", tag="addend")
+            for t in range(PACK):
+                nc.scalar.activation(part_scaled[j][:, t, :], part_b[j][:, t, :], IDENT, scale=high_t[:, 1, t : t + 1])
+
+        def part_inner_sum(j):
+            part_inner[j] = ring.tile([P, PACK, PART], F32, name="inner", tag="inner")
+            nc.vector.tensor_tensor(part_inner[j][:], part_a[j][:], part_scaled[j][:], ADD)
+
+        def part_outer(j):
+            outer = ring.tile([P, PACK, PART], F32, name="outer", tag="outer")
+            nc.vector.tensor_tensor(outer[:], part_b[j][:], part_inner[j][:], MULT)
+            part_woven[j] = held("part_woven%d" % j, [P, PART, PACK], BF16)
+            nc.vector.tensor_tensor(
+                part_woven[j][:], outer[:].rearrange("p t c -> p c t"),
+                low_t[:, 1, :].unsqueeze(1).to_broadcast([P, PART, PACK]), ADD,
+            )
+
+        def part_out(j):
+            tokens = slice(PART * j, PART * (j + 1))
+            codes = held("part_c%d" % j, [P, PART], U32)
+            scales = held("part_s%d" % j, [P, PART], U8)
+            nc.vector.quantize_mx(
+                out=codes[:].bitcast(FP8X4), scales=scales[:], in_=part_woven[j][:].rearrange("p c t -> p (c t)")
+            )
+            acc = bank(3 + j, [P, OUT_TILES, PART])
+            for c in range(OUT_TILES):
+                product_out(acc[:, c, :], 0, c, h_c[0, 1][:, tokens], h_s[0, 1][:, tokens], c == 0, False)
+            for c in range(OUT_TILES):
+                product_out(acc[:, c, :], 1, c, codes[:], scales[:], False, c == OUT_TILES - 1)
+            res = held("part_res%d" % j, [P, OUT_TILES, PART], F32)
+            if j < parts - 1:
+                for c in range(OUT_TILES):
+                    nc.scalar.activation(res[:, c, :], acc[:, c, :], IDENT, bias=bias_t[:, c : c + 1])
+            else:
+                nc.vector.tensor_tensor(res[:], acc[:], bias_t[:].unsqueeze(2).to_broadcast([P, OUT_TILES, PART]), ADD)
+            columns = out[:, HALF + PART * j : HALF + PART * (j + 1)]
+            nc.sync.dma_start(columns.rearrange("(c p) j -> p c j", p=P), res[:])
+
+        for i in range(AHEAD):
+            step_products(i)
+        step_inner(0)
+        for i in range(len(STEPS)):
+            if i == 1:
+                round_w1(1, 0, CAST_PARTS)
+            if i == 2:
+                order_w2(1)
+            if i == 3:
+                round_w1(1, 1, CAST_PARTS)
+                quantise_w1(1, 0)
+            if i == 4:
+                w3_w, w3_s, bias_t = load_w3()
+            if i == LAST_UNIT - AHEAD:
+                quantise_w1(1, 1)
+            if i + AHEAD < len(STEPS):
+                step_products(i + AHEAD)
+            if i + 1 < len(STEPS):
+                step_inner(i + 1)
+            else:
+                part_products(0)
+                part_products(1)
+                part_inner_sum(0)
+            step_outer(i)
+            if i >= PACK and i % PACK in (0, 1):
+                interleave(*UNITS[i // PACK - 1], i % PACK)
+            if i >= PACK and i % PACK in (1, 2):
+                quantise_h(*UNITS[i // PACK - 1], i % PACK - 1)
+
+        interleave(*UNITS[-1], 0)
+        interleave(*UNITS[-1], 1)
+        part_inner_sum(1)
+        part_outer(0)
+        part_products(2)
+        quantise_h(*UNITS[-1], 0)
+        part_outer(1)
+        part_products(3)
+        quantise_h(*UNITS[-1], 1)
+        part_inner_sum(2)
+        for c in range(OUT_TILES):
+            first_half_out(c)
+        part_out(0)
+        part_inner_sum(3)
+        part_outer(2)
+        part_out(1)
+        part_outer(3)
+        part_out(2)
+        part_out(3)

@@ -24,13 +24,14 @@ HALF = 512
 PART = 128
 QUADS = 4
 OUT_TILES = N // P
+SCALE_ROW0 = 96
 AHEAD = 3
 RING = 4
 CAST_PARTS = 4
-UNITS = [(0, 0), (0, 1), (1, 0)]
-STEPS = [(g, s, t) for g, s in UNITS for t in range(PACK)]
-LAST_UNIT = len(STEPS) - PACK
-MIX_BANKS = (2, 7)
+UNITS = [(0, 0, HALF), (0, HALF, HALF)] + [(1, first, HALF // 2) for first in range(0, S - HALF // 2, HALF // 2)]
+STEPS = [(u, t0) for u, unit in enumerate(UNITS) for t0 in range(0, PACK, HALF // unit[2])]
+PART_STARTS = list(range(HALF + HALF // 2, S, PART))
+A_BANKS, B_BANKS, OUT_BANKS = (0, 1), (2, 3, 4, 5), (6, 7)
 
 
 def tile_list_pavement_upstream_horner_kernel(
@@ -58,9 +59,8 @@ def tile_list_pavement_upstream_horner_kernel(
         nc.sync.dma_start(lists[1][:], offs2)
 
         tab_s = held("tab_s", [P, T], U8)
-        nc.sync.dma_start(tab_s[0:32, :].bitcast(I32), tab_scales.rearrange("a q t -> (a q) t").bitcast(I32))
-        nc.vector.memset(tab_s[32:64, :].bitcast(I32), 0)
-        nc.vector.memset(tab_s[64:128, :].bitcast(I32), 0)
+        nc.sync.dma_start(tab_s[SCALE_ROW0:P, :].bitcast(I32), tab_scales.rearrange("a q t -> (a q) t").bitcast(I32))
+        nc.vector.memset(tab_s[0:SCALE_ROW0, :].bitcast(I32), 0)
         w2_s_raw = held("w2_s_raw", [P, 2, H], U8, tag="weight_scales")
         nc.vector.memset(w2_s_raw[:].rearrange("p a c -> p (a c)").bitcast(I32), 0)
         v_s_all = held("v_s_all", [P, 4 * S], U8)
@@ -100,7 +100,7 @@ def tile_list_pavement_upstream_horner_kernel(
             nc.vector.tensor_copy(picked_s[:, S * which : S * (which + 1)], tab_s[:].indirect(lists[which][:]))
         for a in range(2):
             for q in range(QUADS):
-                row = 16 * a + 4 * q
+                row = SCALE_ROW0 + 16 * a + 4 * q
                 nc.sync.dma_start(v_s[a][32 * q : 32 * q + 4, :].bitcast(I32), picked_s[row : row + 4, :].bitcast(I32))
 
         v_w = {}
@@ -128,34 +128,35 @@ def tile_list_pavement_upstream_horner_kernel(
             w1_s[g, a] = held("w1_s%d%d" % (g, a), [P, PASS], U8)
             nc.vector.quantize_mx(out=w1_c[g, a][:].bitcast(FP8X4), scales=w1_s[g, a][:], in_=w1_bf[g, a][:])
 
-        def order_w2(g):
+        def order_w2(g, engine):
             w2_c[g] = held("w2_c%d" % g, [P, 2, PASS], U32)
             w2_s[g] = held("w2_s%d" % g, [P, 2, PASS], U8)
-            nc.vector.tensor_copy(
+            engine.tensor_copy(
                 w2_s[g][:].rearrange("p a (t m) -> p a m t", t=PACK),
                 w2_s_raw[:, :, PASS * g : PASS * (g + 1)].rearrange("p a (m t) -> p a m t", t=PACK),
             )
-            nc.vector.tensor_copy(
+            engine.tensor_copy(
                 w2_c[g][:].bitcast(I32).rearrange("p a (t m) -> p a m t", t=PACK),
                 w2_raw[g][:].bitcast(I32).rearrange("p a (m t) -> p a m t", t=PACK),
             )
 
+        def second_half_words(wanted, tag):
+            late = held("late", [P, len(wanted), HALF], U16, tag=tag)
+            for place, (which, a) in enumerate(wanted):
+                gather_words(which, a, 1, late[:, place, :])
+
         round_w1(0, 0, 1)
         round_w1(0, 1, 1)
-        for s in range(2):
+        for a in range(2):
             for which in range(2):
-                gather_words(which, 0, s, own_room(which, 0, s))
-        for which in (1, 0):
-            gather_words(which, 1, 0, own_room(which, 1, 0))
+                gather_words(which, a, 0, own_room(which, a, 0))
         quantise_w1(0, 0)
-        order_w2(0)
+        order_w2(0, nc.vector)
         quantise_w1(0, 1)
         load_w1(1, 0)
         load_w1(1, 1)
         load_w2(1)
-        late = held("late", [P, 2, HALF], U16, tag="w1_bf01")
-        for which in range(2):
-            gather_words(which, 1, 1, late[:, which, :])
+        second_half_words([(0, 1), (1, 1)], "w1_bf01")
 
         def load_w3():
             words = held("w3_w", [P, 2, N], U16, tag="w1_raw0")
@@ -168,22 +169,16 @@ def tile_list_pavement_upstream_horner_kernel(
                 nc.sync.dma_start(per_row[:], bias.rearrange("(c p) -> p c", p=P))
             return words, scales, per_row
 
-        def product_a(acc, g, s, t, tokens):
+        def product(acc, which, g, t, first, count):
             cols = slice(P * t, P * (t + 1))
+            s, local = divmod(first, HALF)
             for a in range(2):
+                codes = w1_c[g, a][:, cols] if which == 0 else w2_c[g][:, a, cols]
+                scales = w1_s[g, a][:, cols] if which == 0 else w2_s[g][:, a, cols]
                 nc.tensor.matmul_mx(
-                    out=acc, lhsT=w1_c[g, a][:, cols].bitcast(FP8X4), lhsT_scale=w1_s[g, a][:, cols],
-                    rhs=v_w[0, a, s][:, tokens].bitcast(FP4X4), rhs_scale=v_s[a][:, HALF * s : HALF * (s + 1)][:, tokens],
-                    start=(a == 0), stop=(a == 1),
-                )
-
-        def product_b(acc, g, s, t, tokens):
-            cols = slice(P * t, P * (t + 1))
-            for a in range(2):
-                nc.tensor.matmul_mx(
-                    out=acc, lhsT=w2_c[g][:, a, cols].bitcast(FP8X4), lhsT_scale=w2_s[g][:, a, cols],
-                    rhs=v_w[1, a, s][:, tokens].bitcast(FP4X4),
-                    rhs_scale=v_s[a][:, S + HALF * s : S + HALF * (s + 1)][:, tokens],
+                    out=acc, lhsT=codes.bitcast(FP8X4), lhsT_scale=scales,
+                    rhs=v_w[which, a, s][:, local : local + count].bitcast(FP4X4),
+                    rhs_scale=v_s[a][:, S * which + first : S * which + first + count],
                     start=(a == 0), stop=(a == 1),
                 )
 
@@ -194,151 +189,164 @@ def tile_list_pavement_upstream_horner_kernel(
                 rhs=codes.bitcast(FP8X4), rhs_scale=scales, start=start, stop=stop,
             )
 
-        addend, b_bank, inner, slices, woven, h_c, h_s = {}, {}, {}, {}, {}, {}, {}
+        addend, b_bank, inner, pairs, woven, h_c, h_s = {}, {}, {}, {}, {}, {}, {}
 
         def step_products(i):
-            g, s, t = STEPS[i]
-            a_bank = bank(i % 3 if i < LAST_UNIT else i % 2, [P, HALF])
-            product_a(a_bank[:], g, s, t, slice(0, HALF))
-            b_bank[i] = bank(3 + (i % 5 if i < LAST_UNIT else i % 4), [P, HALF])
-            product_b(b_bank[i][:], g, s, t, slice(0, HALF))
-            addend[i] = ring.tile([P, HALF], F32, name="addend", tag="addend")
+            u, t0 = STEPS[i]
+            g, first, count = UNITS[u]
+            shape = [P, HALF // count, count]
+            a_bank = bank(A_BANKS[i % 2], shape)
+            for k in range(shape[1]):
+                product(a_bank[:, k, :], 0, g, t0 + k, first, count)
+            b_bank[i] = bank(B_BANKS[i % 4], shape)
+            for k in range(shape[1]):
+                product(b_bank[i][:, k, :], 1, g, t0 + k, first, count)
+            addend[i] = held("addend%d" % i, shape, F32) if i < 2 else ring.tile(shape, F32, name="addend", tag="addend")
             nc.scalar.copy(addend[i][:], a_bank[:])
 
         def step_inner(i):
-            g, s, t = STEPS[i]
-            inner[i] = ring.tile([P, HALF], F32, name="inner", tag="inner")
-            nc.vector.scalar_tensor_tensor(inner[i][:], b_bank[i][:], high_t[:, g, t : t + 1], addend[i][:], MULT, ADD)
+            u, t0 = STEPS[i]
+            g, first, count = UNITS[u]
+            inner[i] = ring.tile([P, HALF // count, count], F32, name="inner", tag="inner")
+            for k in range(HALF // count):
+                per_row = high_t[:, g, t0 + k : t0 + k + 1]
+                nc.vector.scalar_tensor_tensor(inner[i][:, k, :], b_bank[i][:, k, :], per_row, addend[i][:, k, :], MULT, ADD)
 
         def step_outer(i):
-            g, s, t = STEPS[i]
-            outer = ring.tile([P, HALF], F32, name="outer", tag="outer")
+            u, t0 = STEPS[i]
+            g, first, count = UNITS[u]
+            outer = ring.tile([P, HALF // count, count], F32, name="outer", tag="outer")
             nc.vector.tensor_tensor(outer[:], b_bank[i][:], inner[i][:], MULT)
-            if t == 0:
-                slices[g, s] = ring.tile([P, PACK, HALF], BF16, name="slices", tag="slices")
-            nc.gpsimd.tensor_scalar(slices[g, s][:, t, :], outer[:], 1.0, low_t[:, g, t : t + 1], MULT, ADD)
+            if t0 == 0:
+                pairs[u] = held("pairs%d" % u, [P, 2, count, 2], BF16)
+            for k in range(HALF // count):
+                t = t0 + k
+                nc.gpsimd.tensor_scalar(pairs[u][:, t // 2, :, t % 2], outer[:, k, :], 1.0, low_t[:, g, t : t + 1], MULT, ADD)
 
-        def interleave(g, s, piece):
-            if piece == 0:
-                woven[g, s] = held("woven%d%d" % (g, s), [P, HALF, PACK], BF16)
-            tokens = slice(HALF // 2 * piece, HALF // 2 * (piece + 1))
+        def interleave(u):
+            count = UNITS[u][2]
+            woven[u] = held("woven%d" % u, [P, PACK * count], BF16)
             nc.scalar.copy(
-                woven[g, s][:, tokens, :].rearrange("p (c e) t -> p c t e", e=4),
-                slices[g, s][:, :, tokens].rearrange("p t (c e) -> p c t e", e=4),
+                woven[u][:].bitcast(U32).rearrange("p (c d) -> p c d", d=2),
+                pairs[u][:].rearrange("p d c e -> p (d c e)").bitcast(U32).rearrange("p (d c) -> p c d", d=2),
             )
 
-        def quantise_h(g, s, piece):
-            if piece == 0:
-                h_c[g, s] = held("h_c%d%d" % (g, s), [P, HALF], U32)
-                h_s[g, s] = held("h_s%d%d" % (g, s), [P, HALF], U8)
-            tokens = slice(HALF // 2 * piece, HALF // 2 * (piece + 1))
-            nc.vector.quantize_mx(
-                out=h_c[g, s][:, tokens].bitcast(FP8X4), scales=h_s[g, s][:, tokens],
-                in_=woven[g, s][:, tokens, :].rearrange("p c t -> p (c t)"),
-            )
+        def quantise_h(u):
+            count = UNITS[u][2]
+            h_c[u] = held("h_c%d" % u, [P, count], U32)
+            h_s[u] = held("h_s%d" % u, [P, count], U8)
+            nc.vector.quantize_mx(out=h_c[u][:].bitcast(FP8X4), scales=h_s[u][:], in_=woven[u][:])
 
-        def first_half_out(c):
-            acc = bank(MIX_BANKS[c % 2], [P, HALF])
-            for g in range(2):
-                product_out(acc[:], g, c, h_c[g, 0][:], h_s[g, 0][:], g == 0, g == 1)
-            res = held("res%d" % c, [P, HALF], F32)
-            nc.scalar.activation(res[:], acc[:], IDENT, bias=bias_t[:, c : c + 1])
-            nc.sync.dma_start(out[P * c : P * (c + 1), 0:HALF], res[:])
+        def unit_out(u, half):
+            first, count = UNITS[u][1:]
+            s, local = divmod(first, HALF)
+            tokens = slice(local, local + count)
+            acc = bank(OUT_BANKS[half], [P, 2, count])
+            res = held("res%d%d" % (u, half), [P, 2, count], F32)
+            for e in range(2):
+                product_out(acc[:, e, :], 0, 2 * half + e, h_c[s][:, tokens], h_s[s][:, tokens], e == 0, False)
+            for e in range(2):
+                product_out(acc[:, e, :], 1, 2 * half + e, h_c[u][:], h_s[u][:], False, e == 1)
+            for e in range(2):
+                c = 2 * half + e
+                nc.scalar.activation(res[:, e, :], acc[:, e, :], IDENT, bias=bias_t[:, c : c + 1])
+            rows = out[2 * P * half : 2 * P * (half + 1), first : first + count]
+            nc.sync.dma_start(rows.rearrange("(c p) j -> p c j", p=P), res[:])
 
-        parts = HALF // PART
-        part_a, part_b, part_scaled, part_inner, part_woven = {}, {}, {}, {}, {}
+        part_a, part_b, part_scaled, part_inner, part_outer, part_woven, part_c, part_s = {}, {}, {}, {}, {}, {}, {}, {}
 
         def part_products(j):
-            tokens = slice(PART * j, PART * (j + 1))
-            part_a[j] = bank(j % 2, [P, PACK, PART])
-            part_b[j] = bank(3 + j, [P, PACK, PART])
+            part_a[j] = bank(A_BANKS[(len(STEPS) + j) % 2], [P, PACK, PART])
+            part_b[j] = bank(B_BANKS[(len(STEPS) + j) % 4], [P, PACK, PART])
             for t in range(PACK):
-                product_b(part_b[j][:, t, :], 1, 1, t, tokens)
+                product(part_b[j][:, t, :], 1, 1, t, PART_STARTS[j], PART)
             for t in range(PACK):
-                product_a(part_a[j][:, t, :], 1, 1, t, tokens)
+                product(part_a[j][:, t, :], 0, 1, t, PART_STARTS[j], PART)
             part_scaled[j] = ring.tile([P, PACK, PART], F32, name="addend", tag="addend")
             for t in range(PACK):
                 nc.scalar.activation(part_scaled[j][:, t, :], part_b[j][:, t, :], IDENT, scale=high_t[:, 1, t : t + 1])
 
-        def part_inner_sum(j):
+        def part_sum(j):
             part_inner[j] = ring.tile([P, PACK, PART], F32, name="inner", tag="inner")
             nc.vector.tensor_tensor(part_inner[j][:], part_a[j][:], part_scaled[j][:], ADD)
 
-        def part_outer(j):
-            outer = ring.tile([P, PACK, PART], F32, name="outer", tag="outer")
-            nc.vector.tensor_tensor(outer[:], part_b[j][:], part_inner[j][:], MULT)
+        def part_times_b(j):
+            part_outer[j] = ring.tile([P, PACK, PART], F32, name="outer", tag="outer")
+            nc.vector.tensor_tensor(part_outer[j][:], part_b[j][:], part_inner[j][:], MULT)
+
+        def part_weave(j):
             part_woven[j] = held("part_woven%d" % j, [P, PART, PACK], BF16)
             nc.vector.tensor_tensor(
-                part_woven[j][:], outer[:].rearrange("p t c -> p c t"),
-                low_t[:, 1, :].unsqueeze(1).to_broadcast([P, PART, PACK]), ADD,
+                part_woven[j][:].rearrange("p (c e) t -> p c t e", e=4),
+                part_outer[j][:].rearrange("p t (c e) -> p c t e", e=4),
+                low_t[:, 1, :].unsqueeze(1).unsqueeze(3).to_broadcast([P, PART // 4, PACK, 4]), ADD,
+            )
+
+        def part_quantise(j):
+            part_c[j] = held("part_c%d" % j, [P, PART], U32)
+            part_s[j] = held("part_s%d" % j, [P, PART], U8)
+            nc.vector.quantize_mx(
+                out=part_c[j][:].bitcast(FP8X4), scales=part_s[j][:], in_=part_woven[j][:].rearrange("p c t -> p (c t)")
             )
 
         def part_out(j):
-            tokens = slice(PART * j, PART * (j + 1))
-            codes = held("part_c%d" % j, [P, PART], U32)
-            scales = held("part_s%d" % j, [P, PART], U8)
-            nc.vector.quantize_mx(
-                out=codes[:].bitcast(FP8X4), scales=scales[:], in_=part_woven[j][:].rearrange("p c t -> p (c t)")
-            )
-            acc = bank(3 + j, [P, OUT_TILES, PART])
+            local = slice(PART_STARTS[j] - HALF, PART_STARTS[j] - HALF + PART)
+            acc = bank(B_BANKS[(len(STEPS) + 2 + j) % 4], [P, OUT_TILES, PART])
             for c in range(OUT_TILES):
-                product_out(acc[:, c, :], 0, c, h_c[0, 1][:, tokens], h_s[0, 1][:, tokens], c == 0, False)
+                product_out(acc[:, c, :], 0, c, h_c[1][:, local], h_s[1][:, local], c == 0, False)
             for c in range(OUT_TILES):
-                product_out(acc[:, c, :], 1, c, codes[:], scales[:], False, c == OUT_TILES - 1)
+                product_out(acc[:, c, :], 1, c, part_c[j][:], part_s[j][:], False, c == OUT_TILES - 1)
             res = held("part_res%d" % j, [P, OUT_TILES, PART], F32)
-            if j < parts - 1:
+            if j == 0:
                 for c in range(OUT_TILES):
                     nc.scalar.activation(res[:, c, :], acc[:, c, :], IDENT, bias=bias_t[:, c : c + 1])
             else:
                 nc.vector.tensor_tensor(res[:], acc[:], bias_t[:].unsqueeze(2).to_broadcast([P, OUT_TILES, PART]), ADD)
-            columns = out[:, HALF + PART * j : HALF + PART * (j + 1)]
+            columns = out[:, PART_STARTS[j] : PART_STARTS[j] + PART]
             nc.sync.dma_start(columns.rearrange("(c p) j -> p c j", p=P), res[:])
 
         for i in range(AHEAD):
             step_products(i)
         step_inner(0)
+        second_half_words([(0, 0)], "addend0")
         for i in range(len(STEPS)):
-            if i == 1:
+            u = STEPS[i][0]
+            if i + AHEAD == 2 * PACK:
                 round_w1(1, 0, CAST_PARTS)
-            if i == 2:
-                order_w2(1)
-            if i == 3:
                 round_w1(1, 1, CAST_PARTS)
+                order_w2(1, nc.vector)
                 quantise_w1(1, 0)
-            if i == 4:
-                w3_w, w3_s, bias_t = load_w3()
-            if i == LAST_UNIT - AHEAD:
                 quantise_w1(1, 1)
+                w3_w, w3_s, bias_t = load_w3()
+            if i == 1:
+                second_half_words([(1, 0)], "addend1")
             if i + AHEAD < len(STEPS):
                 step_products(i + AHEAD)
+            elif i + AHEAD - len(STEPS) < len(PART_STARTS):
+                part_products(i + AHEAD - len(STEPS))
             if i + 1 < len(STEPS):
                 step_inner(i + 1)
             else:
-                part_products(0)
-                part_products(1)
-                part_inner_sum(0)
+                part_sum(0)
             step_outer(i)
-            if i >= PACK and i % PACK in (0, 1):
-                interleave(*UNITS[i // PACK - 1], i % PACK)
-            if i >= PACK and i % PACK in (1, 2):
-                quantise_h(*UNITS[i // PACK - 1], i % PACK - 1)
+            if i + 1 == len(STEPS) or STEPS[i + 1][0] != u:
+                interleave(u)
+            if i >= 2 and STEPS[i - 2][0] != STEPS[i - 1][0]:
+                done = STEPS[i - 2][0]
+                quantise_h(done)
+                if UNITS[done][0] == 1:
+                    unit_out(done, 0)
+                    unit_out(done, 1)
 
-        interleave(*UNITS[-1], 0)
-        interleave(*UNITS[-1], 1)
-        part_inner_sum(1)
-        part_outer(0)
-        part_products(2)
-        quantise_h(*UNITS[-1], 0)
-        part_outer(1)
-        part_products(3)
-        quantise_h(*UNITS[-1], 1)
-        part_inner_sum(2)
-        for c in range(OUT_TILES):
-            first_half_out(c)
+        part_sum(1)
+        part_times_b(0)
+        part_times_b(1)
+        quantise_h(len(UNITS) - 1)
+        part_weave(0)
+        unit_out(len(UNITS) - 1, 0)
+        unit_out(len(UNITS) - 1, 1)
+        part_weave(1)
+        part_quantise(0)
+        part_quantise(1)
         part_out(0)
-        part_inner_sum(3)
-        part_outer(2)
         part_out(1)
-        part_outer(3)
-        part_out(2)
-        part_out(3)

@@ -26,11 +26,15 @@ QUADS = 4
 OUT_TILES = N // P
 SCALE_ROW0 = 96
 AHEAD = 3
+A_AHEAD = 4
 RING = 4
 CAST_PARTS = 4
-UNITS = [(0, 0, HALF), (0, HALF, HALF)] + [(1, first, HALF // 2) for first in range(0, S - HALF // 2, HALF // 2)]
+QUARTER = HALF // 2
+UNITS = [(0, 0, HALF), (0, HALF + QUARTER, QUARTER), (1, 0, QUARTER), (1, QUARTER, QUARTER), (0, HALF, QUARTER), (1, HALF, QUARTER)]
+GROUP0_UNIT = {0: 0, QUARTER: 0, HALF: 4}
 STEPS = [(u, t0) for u, unit in enumerate(UNITS) for t0 in range(0, PACK, HALF // unit[2])]
 PART_STARTS = list(range(HALF + HALF // 2, S, PART))
+QUANTISE_AT = {8: (0, 1), 10: (2,), 12: (3,)}
 A_BANKS, B_BANKS, OUT_BANKS = (0, 1), (2, 3, 4, 5), (6, 7)
 
 
@@ -55,22 +59,17 @@ def tile_list_pavement_upstream_horner_kernel(
                 nc.sync.dma_start(tile[32 * q : 32 * q + 4, :, :].bitcast(I32), rows.bitcast(I32))
 
         lists = [held("list_a", [P, S // 16], U16), held("list_b", [P, S // 16], U16)]
-        nc.sync.dma_start(lists[0][:], offs)
-        nc.sync.dma_start(lists[1][:], offs2)
-
+        w2_s_raw = held("w2_s_raw", [P, 2, H], U8)
+        nc.gpsimd.memset(w2_s_raw[:].rearrange("p a c -> p (a c)").bitcast(I32), 0)
         tab_s = held("tab_s", [P, T], U8)
+        nc.sync.dma_start(lists[0][:], offs)
         nc.sync.dma_start(tab_s[SCALE_ROW0:P, :].bitcast(I32), tab_scales.rearrange("a q t -> (a q) t").bitcast(I32))
+        nc.sync.dma_start(lists[1][:], offs2)
+        load_scale_rows(w2_s_raw, w2_scales)
         nc.vector.memset(tab_s[0:SCALE_ROW0, :].bitcast(I32), 0)
-        w2_s_raw = held("w2_s_raw", [P, 2, H], U8, tag="weight_scales")
-        nc.vector.memset(w2_s_raw[:].rearrange("p a c -> p (a c)").bitcast(I32), 0)
         v_s_all = held("v_s_all", [P, 4 * S], U8)
         nc.gpsimd.memset(v_s_all[:].bitcast(I32), 0)
         v_s = [v_s_all[:, 2 * S * a : 2 * S * (a + 1)] for a in range(2)]
-
-        high_t = held("high_t", [P, 2, PACK], F32)
-        low_t = held("low_t", [P, 2, PACK], F32)
-        nc.sync.dma_start(high_t[:], high.rearrange("(g p t) -> p g t", g=2, t=PACK))
-        nc.sync.dma_start(low_t[:], low.rearrange("(g p t) -> p g t", g=2, t=PACK))
 
         tab_w = [held("tab_w%d" % a, [P, T], U16) for a in range(2)]
         w1_raw, w2_raw = {}, {}
@@ -78,30 +77,36 @@ def tile_list_pavement_upstream_horner_kernel(
         def load_tab(a):
             nc.sync.dma_start(tab_w[a][:].bitcast(I32), tab_words[a].bitcast(I32))
 
-        def load_w1(g, a):
-            w1_raw[g, a] = held("w1_raw", [P, PACK, PASS], F32, tag="w1_raw%d" % a)
+        def load_w1(g, a, room):
+            w1_raw[g, a] = room
             rows = w1[PASS * a : PASS * (a + 1), PASS * g : PASS * (g + 1)]
-            nc.sync.dma_start(w1_raw[g, a][:], rows.rearrange("(p i) c -> p i c", i=PACK))
+            nc.sync.dma_start(room, rows.rearrange("(p i) c -> p i c", i=PACK))
 
-        def load_w2(g):
-            w2_raw[g] = keep.tile([P, 2, PASS], U32, name="w2_raw", tag="w2_raw")
+        def w1_room(tag):
+            return held("w1_raw", [P, PACK, PASS], F32, tag=tag)[:]
+
+        def load_w2(g, room):
+            w2_raw[g] = room
             words = w2_words.rearrange("a p c i -> p a (c i)")[:, :, PACK * PASS * g : PACK * PASS * (g + 1)]
-            nc.sync.dma_start(w2_raw[g][:].bitcast(I32), words.bitcast(I32))
+            nc.sync.dma_start(room, words.bitcast(I32))
 
         load_tab(0)
-        load_w1(0, 0)
+        load_w1(0, 0, w1_room("w1_raw0"))
         load_tab(1)
-        load_scale_rows(w2_s_raw, w2_scales)
-        load_w1(0, 1)
-        load_w2(0)
+        load_w1(0, 1, w1_room("w1_raw1"))
 
         picked_s = held("picked_s", [P, 2 * S], U8)
         for which in range(2):
             nc.vector.tensor_copy(picked_s[:, S * which : S * (which + 1)], tab_s[:].indirect(lists[which][:]))
-        for a in range(2):
+
+        def move_scale_rows(a):
             for q in range(QUADS):
                 row = SCALE_ROW0 + 16 * a + 4 * q
                 nc.sync.dma_start(v_s[a][32 * q : 32 * q + 4, :].bitcast(I32), picked_s[row : row + 4, :].bitcast(I32))
+
+        move_scale_rows(0)
+        load_w1(1, 0, w1_room("tab_s"))
+        move_scale_rows(1)
 
         v_w = {}
 
@@ -118,7 +123,7 @@ def tile_list_pavement_upstream_horner_kernel(
         def round_w1(g, a, parts):
             w1_bf[g, a] = held("w1_bf", [P, PACK * PASS], BF16, tag="w1_bf%d%d" % (g, a))
             dst = w1_bf[g, a][:].rearrange("p (t m i) -> p m i t", t=PACK, i=PACK)
-            src = w1_raw[g, a][:].rearrange("p i (m t) -> p m i t", t=PACK)
+            src = w1_raw[g, a].rearrange("p i (m t) -> p m i t", t=PACK)
             for part in range(parts):
                 ms = slice(P // parts * part, P // parts * (part + 1))
                 nc.scalar.copy(dst[:, ms, :, :], src[:, ms, :, :])
@@ -128,16 +133,19 @@ def tile_list_pavement_upstream_horner_kernel(
             w1_s[g, a] = held("w1_s%d%d" % (g, a), [P, PASS], U8)
             nc.vector.quantize_mx(out=w1_c[g, a][:].bitcast(FP8X4), scales=w1_s[g, a][:], in_=w1_bf[g, a][:])
 
-        def order_w2(g, engine):
-            w2_c[g] = held("w2_c%d" % g, [P, 2, PASS], U32)
+        def order_w2_scales(g):
             w2_s[g] = held("w2_s%d" % g, [P, 2, PASS], U8)
-            engine.tensor_copy(
-                w2_s[g][:].rearrange("p a (t m) -> p a m t", t=PACK),
-                w2_s_raw[:, :, PASS * g : PASS * (g + 1)].rearrange("p a (m t) -> p a m t", t=PACK),
-            )
-            engine.tensor_copy(
+            for a in range(2):
+                nc.gpsimd.tensor_copy(
+                    w2_s[g][:, a, :].rearrange("p (t m) -> p t m", t=PACK),
+                    w2_s_raw[:, a, PASS * g : PASS * (g + 1)].rearrange("p (m t) -> p t m", t=PACK),
+                )
+
+        def order_w2_words(g):
+            w2_c[g] = held("w2_c%d" % g, [P, 2, PASS], U32)
+            nc.vector.tensor_copy(
                 w2_c[g][:].bitcast(I32).rearrange("p a (t m) -> p a m t", t=PACK),
-                w2_raw[g][:].bitcast(I32).rearrange("p a (m t) -> p a m t", t=PACK),
+                w2_raw[g].rearrange("p a (m t) -> p a m t", t=PACK),
             )
 
         def second_half_words(wanted, tag):
@@ -146,28 +154,39 @@ def tile_list_pavement_upstream_horner_kernel(
                 gather_words(which, a, 1, late[:, place, :])
 
         round_w1(0, 0, 1)
+        load_w2(0, held("w2_raw", [P, 2, PASS], I32, tag="w1_raw0")[:])
         round_w1(0, 1, 1)
+        round_w1(1, 0, 1)
         for a in range(2):
             for which in range(2):
                 gather_words(which, a, 0, own_room(which, a, 0))
+        for which in range(2):
+            gather_words(which, 0, 1, own_room(which, 0, 1))
+        order_w2_scales(0)
+        order_w2_scales(1)
         quantise_w1(0, 0)
-        order_w2(0, nc.vector)
         quantise_w1(0, 1)
-        load_w1(1, 0)
-        load_w1(1, 1)
-        load_w2(1)
-        second_half_words([(0, 1), (1, 1)], "w1_bf01")
+        order_w2_words(0)
+        third = held("third", [P, PACK * PASS + 24], F32, tag="w1_raw1")
+        load_w1(1, 1, third[:, 0 : PACK * PASS].rearrange("p (i c) -> p i c", i=PACK))
+        per_row = third[:, PACK * PASS :].rearrange("p (v c) -> p v c", c=8)
+        high_t = per_row[:, 0, :].rearrange("p (g t) -> p g t", g=2)
+        low_t = per_row[:, 1, :].rearrange("p (g t) -> p g t", g=2)
+        bias_t = per_row[:, 2, 0:OUT_TILES]
+        nc.sync.dma_start(high_t, high.rearrange("(g p t) -> p g t", g=2, t=PACK))
+        nc.sync.dma_start(low_t, low.rearrange("(g p t) -> p g t", g=2, t=PACK))
+        with nc.allow_non_contiguous_dma("the bias has one value for each partition of an output tile"):
+            nc.sync.dma_start(bias_t, bias.rearrange("(c p) -> p c", p=P))
+        load_w2(1, held("w2_raw", [P, 2, PASS], I32, tag="tab_s")[:])
+        second_half_words([(0, 1), (1, 1)], "w1_raw0")
 
         def load_w3():
-            words = held("w3_w", [P, 2, N], U16, tag="w1_raw0")
-            scales = held("w3_s", [P, 2, N], U8, tag="weight_scales")
+            words = held("w3_w", [P, 2, N], U16, tag="tab_s")
+            scales = held("w3_s", [P, 2, N], U8, tag="w1_bf10")
             nc.gpsimd.memset(scales[:].rearrange("p a c -> p (a c)").bitcast(I32), 0)
             nc.sync.dma_start(words[:].bitcast(I32), w3_words.rearrange("a p b -> p a b").bitcast(I32))
             load_scale_rows(scales, w3_scales)
-            per_row = held("bias_t", [P, OUT_TILES], F32, tag="w1_raw1")
-            with nc.allow_non_contiguous_dma("the bias has one value for each partition of an output tile"):
-                nc.sync.dma_start(per_row[:], bias.rearrange("(c p) -> p c", p=P))
-            return words, scales, per_row
+            return words, scales
 
         def product(acc, which, g, t, first, count):
             cols = slice(P * t, P * (t + 1))
@@ -189,20 +208,24 @@ def tile_list_pavement_upstream_horner_kernel(
                 rhs=codes.bitcast(FP8X4), rhs_scale=scales, start=start, stop=stop,
             )
 
-        addend, b_bank, inner, pairs, woven, h_c, h_s = {}, {}, {}, {}, {}, {}, {}
+        addend, a_bank, b_bank, inner, slices, woven, h_c, h_s = {}, {}, {}, {}, {}, {}, {}, {}
 
         def step_products(i):
             u, t0 = STEPS[i]
             g, first, count = UNITS[u]
             shape = [P, HALF // count, count]
-            a_bank = bank(A_BANKS[i % 2], shape)
-            for k in range(shape[1]):
-                product(a_bank[:, k, :], 0, g, t0 + k, first, count)
             b_bank[i] = bank(B_BANKS[i % 4], shape)
             for k in range(shape[1]):
                 product(b_bank[i][:, k, :], 1, g, t0 + k, first, count)
-            addend[i] = held("addend%d" % i, shape, F32) if i < 2 else ring.tile(shape, F32, name="addend", tag="addend")
-            nc.scalar.copy(addend[i][:], a_bank[:])
+
+        def step_addend(i):
+            u, t0 = STEPS[i]
+            g, first, count = UNITS[u]
+            a_bank[i] = bank(A_BANKS[i % 2], [P, HALF // count, count])
+            for k in range(HALF // count):
+                product(a_bank[i][:, k, :], 0, g, t0 + k, first, count)
+            addend[i] = ring.tile([P, HALF // count, count], F32, name="addend", tag="addend", bufs=A_AHEAD + 2)
+            nc.scalar.copy(addend[i][:], a_bank[i][:])
 
         def step_inner(i):
             u, t0 = STEPS[i]
@@ -218,18 +241,25 @@ def tile_list_pavement_upstream_horner_kernel(
             outer = ring.tile([P, HALF // count, count], F32, name="outer", tag="outer")
             nc.vector.tensor_tensor(outer[:], b_bank[i][:], inner[i][:], MULT)
             if t0 == 0:
-                pairs[u] = held("pairs%d" % u, [P, 2, count, 2], BF16)
+                slices[u] = held("slices%d" % u, [P, PACK, count], BF16)
             for k in range(HALF // count):
                 t = t0 + k
-                nc.gpsimd.tensor_scalar(pairs[u][:, t // 2, :, t % 2], outer[:, k, :], 1.0, low_t[:, g, t : t + 1], MULT, ADD)
+                if u == 0:
+                    nc.gpsimd.tensor_scalar(slices[u][:, t, :], outer[:, k, :], 1.0, low_t[:, g, t : t + 1], MULT, ADD)
+                else:
+                    nc.scalar.activation(slices[u][:, t, :], outer[:, k, :], IDENT, bias=low_t[:, g, t : t + 1])
 
         def interleave(u):
             count = UNITS[u][2]
-            woven[u] = held("woven%d" % u, [P, PACK * count], BF16)
-            nc.scalar.copy(
-                woven[u][:].bitcast(U32).rearrange("p (c d) -> p c d", d=2),
-                pairs[u][:].rearrange("p d c e -> p (d c e)").bitcast(U32).rearrange("p (d c) -> p c d", d=2),
-            )
+            woven[u] = held("woven", [P, PACK * count], BF16, tag="woven%d" % (u in (1, 5)))
+            if u == len(UNITS) - 1:
+                nc.scalar.copy(
+                    woven[u][:].rearrange("p (c e t) -> p c t e", e=4, t=PACK), slices[u][:].rearrange("p t (c e) -> p c t e", e=4)
+                )
+            else:
+                nc.gpsimd.tensor_scalar(
+                    woven[u][:].rearrange("p (c t) -> p c t", t=PACK), slices[u][:].rearrange("p t c -> p c t"), 1.0, 0.0, MULT, ADD
+                )
 
         def quantise_h(u):
             count = UNITS[u][2]
@@ -237,20 +267,21 @@ def tile_list_pavement_upstream_horner_kernel(
             h_s[u] = held("h_s%d" % u, [P, count], U8)
             nc.vector.quantize_mx(out=h_c[u][:].bitcast(FP8X4), scales=h_s[u][:], in_=woven[u][:])
 
-        def unit_out(u, half):
+        def unit_out(u, half, banks):
             first, count = UNITS[u][1:]
-            s, local = divmod(first, HALF)
-            tokens = slice(local, local + count)
-            acc = bank(OUT_BANKS[half], [P, 2, count])
-            res = held("res%d%d" % (u, half), [P, 2, count], F32)
-            for e in range(2):
-                product_out(acc[:, e, :], 0, 2 * half + e, h_c[s][:, tokens], h_s[s][:, tokens], e == 0, False)
-            for e in range(2):
-                product_out(acc[:, e, :], 1, 2 * half + e, h_c[u][:], h_s[u][:], False, e == 1)
-            for e in range(2):
-                c = 2 * half + e
+            base = GROUP0_UNIT[first]
+            tokens = slice(first - UNITS[base][1], first - UNITS[base][1] + count)
+            per = HALF // count
+            acc = bank(banks[half % 2], [P, per, count])
+            res = held("res%d%d" % (u, half), [P, per, count], F32)
+            for e in range(per):
+                product_out(acc[:, e, :], 0, per * half + e, h_c[base][:, tokens], h_s[base][:, tokens], e == 0, False)
+            for e in range(per):
+                product_out(acc[:, e, :], 1, per * half + e, h_c[u][:], h_s[u][:], False, e == per - 1)
+            for e in range(per):
+                c = per * half + e
                 nc.scalar.activation(res[:, e, :], acc[:, e, :], IDENT, bias=bias_t[:, c : c + 1])
-            rows = out[2 * P * half : 2 * P * (half + 1), first : first + count]
+            rows = out[per * P * half : per * P * (half + 1), first : first + count]
             nc.sync.dma_start(rows.rearrange("(c p) j -> p c j", p=P), res[:])
 
         part_a, part_b, part_scaled, part_inner, part_outer, part_woven, part_c, part_s = {}, {}, {}, {}, {}, {}, {}, {}
@@ -262,7 +293,9 @@ def tile_list_pavement_upstream_horner_kernel(
                 product(part_b[j][:, t, :], 1, 1, t, PART_STARTS[j], PART)
             for t in range(PACK):
                 product(part_a[j][:, t, :], 0, 1, t, PART_STARTS[j], PART)
-            part_scaled[j] = ring.tile([P, PACK, PART], F32, name="addend", tag="addend")
+
+        def part_scale(j):
+            part_scaled[j] = ring.tile([P, PACK, PART], F32, name="addend", tag="addend", bufs=A_AHEAD + 2)
             for t in range(PACK):
                 nc.scalar.activation(part_scaled[j][:, t, :], part_b[j][:, t, :], IDENT, scale=high_t[:, 1, t : t + 1])
 
@@ -275,7 +308,7 @@ def tile_list_pavement_upstream_horner_kernel(
             nc.vector.tensor_tensor(part_outer[j][:], part_b[j][:], part_inner[j][:], MULT)
 
         def part_weave(j):
-            part_woven[j] = held("part_woven%d" % j, [P, PART, PACK], BF16)
+            part_woven[j] = held("part_woven", [P, PART, PACK], BF16, tag="part_woven%d" % j)
             nc.vector.tensor_tensor(
                 part_woven[j][:].rearrange("p (c e) t -> p c t e", e=4),
                 part_outer[j][:].rearrange("p t (c e) -> p c t e", e=4),
@@ -290,61 +323,64 @@ def tile_list_pavement_upstream_horner_kernel(
             )
 
         def part_out(j):
-            local = slice(PART_STARTS[j] - HALF, PART_STARTS[j] - HALF + PART)
+            local = slice(PART * j, PART * (j + 1))
             acc = bank(B_BANKS[(len(STEPS) + 2 + j) % 4], [P, OUT_TILES, PART])
             for c in range(OUT_TILES):
                 product_out(acc[:, c, :], 0, c, h_c[1][:, local], h_s[1][:, local], c == 0, False)
             for c in range(OUT_TILES):
                 product_out(acc[:, c, :], 1, c, part_c[j][:], part_s[j][:], False, c == OUT_TILES - 1)
             res = held("part_res%d" % j, [P, OUT_TILES, PART], F32)
-            if j == 0:
-                for c in range(OUT_TILES):
-                    nc.scalar.activation(res[:, c, :], acc[:, c, :], IDENT, bias=bias_t[:, c : c + 1])
-            else:
-                nc.vector.tensor_tensor(res[:], acc[:], bias_t[:].unsqueeze(2).to_broadcast([P, OUT_TILES, PART]), ADD)
+            nc.vector.tensor_tensor(res[:], acc[:], bias_t.unsqueeze(2).to_broadcast([P, OUT_TILES, PART]), ADD)
             columns = out[:, PART_STARTS[j] : PART_STARTS[j] + PART]
             nc.sync.dma_start(columns.rearrange("(c p) j -> p c j", p=P), res[:])
 
-        for i in range(AHEAD):
-            step_products(i)
+        for i in range(A_AHEAD):
+            step_addend(i)
+            if i < AHEAD:
+                step_products(i)
+        quantise_w1(1, 0)
         step_inner(0)
-        second_half_words([(0, 0)], "addend0")
         for i in range(len(STEPS)):
             u = STEPS[i][0]
-            if i + AHEAD == 2 * PACK:
-                round_w1(1, 0, CAST_PARTS)
-                round_w1(1, 1, CAST_PARTS)
-                order_w2(1, nc.vector)
-                quantise_w1(1, 0)
-                quantise_w1(1, 1)
-                w3_w, w3_s, bias_t = load_w3()
             if i == 1:
-                second_half_words([(1, 0)], "addend1")
+                round_w1(1, 1, CAST_PARTS)
+                quantise_w1(1, 1)
+            if i + 2 == len(STEPS):
+                part_scale(0)
+            if i == 2:
+                order_w2_words(1)
+                w3_w, w3_s = load_w3()
             if i + AHEAD < len(STEPS):
                 step_products(i + AHEAD)
             elif i + AHEAD - len(STEPS) < len(PART_STARTS):
                 part_products(i + AHEAD - len(STEPS))
             if i + 1 < len(STEPS):
                 step_inner(i + 1)
-            else:
-                part_sum(0)
             step_outer(i)
-            if i + 1 == len(STEPS) or STEPS[i + 1][0] != u:
-                interleave(u)
-            if i >= 2 and STEPS[i - 2][0] != STEPS[i - 1][0]:
-                done = STEPS[i - 2][0]
+            if i + A_AHEAD < len(STEPS):
+                step_addend(i + A_AHEAD)
+            for done in QUANTISE_AT.get(i, ()):
                 quantise_h(done)
-                if UNITS[done][0] == 1:
-                    unit_out(done, 0)
-                    unit_out(done, 1)
+            if i in (3, 5):
+                interleave(u)
+            if i in (8, 10, 12):
+                interleave(i // 2 - 2)
+            if i in (11, 12):
+                unit_out(2, i - 11, OUT_BANKS)
 
+        part_scale(1)
+        interleave(5)
+        part_sum(0)
         part_sum(1)
+        unit_out(3, 0, OUT_BANKS)
+        unit_out(3, 1, OUT_BANKS)
         part_times_b(0)
         part_times_b(1)
-        quantise_h(len(UNITS) - 1)
+        quantise_h(4)
+        quantise_h(5)
         part_weave(0)
-        unit_out(len(UNITS) - 1, 0)
-        unit_out(len(UNITS) - 1, 1)
+        unit_out(5, 0, A_BANKS)
+        unit_out(5, 1, A_BANKS)
         part_weave(1)
         part_quantise(0)
         part_quantise(1)

@@ -26,15 +26,17 @@ QUADS = 4
 OUT_TILES = N // P
 SCALE_ROW0 = 96
 AHEAD = 3
-A_AHEAD = 4
+A_AHEAD = 5
 RING = 4
 CAST_PARTS = 4
 QUARTER = HALF // 2
-UNITS = [(0, 0, HALF), (0, HALF + QUARTER, QUARTER), (1, 0, QUARTER), (1, QUARTER, QUARTER), (0, HALF, QUARTER), (1, HALF, QUARTER)]
-GROUP0_UNIT = {0: 0, QUARTER: 0, HALF: 4}
+UNITS = [(0, 0, HALF), (0, HALF, QUARTER), (1, 0, QUARTER), (1, QUARTER, QUARTER), (1, HALF, QUARTER), (0, HALF + QUARTER, QUARTER)]
+PART_STARTS = list(range(HALF + QUARTER, S, PART))
+UNITS = UNITS + [(1, first, PART) for first in PART_STARTS]
+GROUP0_UNIT = {0: 0, QUARTER: 0, HALF: 1}
 STEPS = [(u, t0) for u, unit in enumerate(UNITS) for t0 in range(0, PACK, HALF // unit[2])]
-PART_STARTS = list(range(HALF + HALF // 2, S, PART))
-QUANTISE_AT = {8: (0, 1), 10: (2,), 12: (3,)}
+INTERLEAVE_AT = {3: (0,), 5: (1,), 7: (2,), 9: (3,), 11: (4,), 13: (5,)}
+QUANTISE_AT = {7: (0, 1), 9: (2,), 11: (3,), 13: (4,)}
 A_BANKS, B_BANKS, OUT_BANKS = (0, 1), (2, 3, 4, 5), (6, 7)
 
 
@@ -66,6 +68,8 @@ def tile_list_pavement_upstream_horner_kernel(
         nc.sync.dma_start(tab_s[SCALE_ROW0:P, :].bitcast(I32), tab_scales.rearrange("a q t -> (a q) t").bitcast(I32))
         nc.sync.dma_start(lists[1][:], offs2)
         load_scale_rows(w2_s_raw, w2_scales)
+        w3_s = held("w3_s", [P, 2, N], U8)
+        nc.gpsimd.memset(w3_s[:].rearrange("p a c -> p (a c)").bitcast(I32), 0)
         nc.vector.memset(tab_s[0:SCALE_ROW0, :].bitcast(I32), 0)
         v_s_all = held("v_s_all", [P, 4 * S], U8)
         nc.gpsimd.memset(v_s_all[:].bitcast(I32), 0)
@@ -91,6 +95,7 @@ def tile_list_pavement_upstream_horner_kernel(
             nc.sync.dma_start(room, words.bitcast(I32))
 
         load_tab(0)
+        load_scale_rows(w3_s, w3_scales)
         load_w1(0, 0, w1_room("w1_raw0"))
         load_tab(1)
         load_w1(0, 1, w1_room("w1_raw1"))
@@ -129,7 +134,7 @@ def tile_list_pavement_upstream_horner_kernel(
                 nc.scalar.copy(dst[:, ms, :, :], src[:, ms, :, :])
 
         def quantise_w1(g, a):
-            w1_c[g, a] = held("w1_c%d%d" % (g, a), [P, PASS], U32)
+            w1_c[g, a] = held("w1_c%d%d" % (g, a), [P, PASS], U32, tag="w1_raw0" if (g, a) == (1, 0) else None)
             w1_s[g, a] = held("w1_s%d%d" % (g, a), [P, PASS], U8)
             nc.vector.quantize_mx(out=w1_c[g, a][:].bitcast(FP8X4), scales=w1_s[g, a][:], in_=w1_bf[g, a][:])
 
@@ -143,10 +148,17 @@ def tile_list_pavement_upstream_horner_kernel(
 
         def order_w2_words(g):
             w2_c[g] = held("w2_c%d" % g, [P, 2, PASS], U32)
-            nc.vector.tensor_copy(
-                w2_c[g][:].bitcast(I32).rearrange("p a (t m) -> p a m t", t=PACK),
-                w2_raw[g].rearrange("p a (m t) -> p a m t", t=PACK),
-            )
+            if g == 1:
+                nc.vector.tensor_copy(
+                    w2_c[g][:].bitcast(I32).rearrange("p a (t m) -> p a m t", t=PACK),
+                    w2_raw[g].rearrange("p a (m t) -> p a m t", t=PACK),
+                )
+                return
+            for t in range(PACK):
+                nc.gpsimd.tensor_copy(
+                    w2_c[g][:].bitcast(I32).rearrange("p a (t m) -> p a t m", t=PACK)[:, :, t, :],
+                    w2_raw[g].rearrange("p a (m t) -> p a t m", t=PACK)[:, :, t, :],
+                )
 
         def second_half_words(wanted, tag):
             late = held("late", [P, len(wanted), HALF], U16, tag=tag)
@@ -168,7 +180,6 @@ def tile_list_pavement_upstream_horner_kernel(
         quantise_w1(0, 1)
         order_w2_words(0)
         third = held("third", [P, PACK * PASS + 24], F32, tag="w1_raw1")
-        load_w1(1, 1, third[:, 0 : PACK * PASS].rearrange("p (i c) -> p i c", i=PACK))
         per_row = third[:, PACK * PASS :].rearrange("p (v c) -> p v c", c=8)
         high_t = per_row[:, 0, :].rearrange("p (g t) -> p g t", g=2)
         low_t = per_row[:, 1, :].rearrange("p (g t) -> p g t", g=2)
@@ -177,16 +188,14 @@ def tile_list_pavement_upstream_horner_kernel(
         nc.sync.dma_start(low_t, low.rearrange("(g p t) -> p g t", g=2, t=PACK))
         with nc.allow_non_contiguous_dma("the bias has one value for each partition of an output tile"):
             nc.sync.dma_start(bias_t, bias.rearrange("(c p) -> p c", p=P))
+        load_w1(1, 1, third[:, 0 : PACK * PASS].rearrange("p (i c) -> p i c", i=PACK))
         load_w2(1, held("w2_raw", [P, 2, PASS], I32, tag="tab_s")[:])
-        second_half_words([(0, 1), (1, 1)], "w1_raw0")
+        second_half_words([(0, 1), (1, 1)], "w1_bf01")
 
         def load_w3():
             words = held("w3_w", [P, 2, N], U16, tag="tab_s")
-            scales = held("w3_s", [P, 2, N], U8, tag="w1_bf10")
-            nc.gpsimd.memset(scales[:].rearrange("p a c -> p (a c)").bitcast(I32), 0)
             nc.sync.dma_start(words[:].bitcast(I32), w3_words.rearrange("a p b -> p a b").bitcast(I32))
-            load_scale_rows(scales, w3_scales)
-            return words, scales
+            return words
 
         def product(acc, which, g, t, first, count):
             cols = slice(P * t, P * (t + 1))
@@ -208,7 +217,7 @@ def tile_list_pavement_upstream_horner_kernel(
                 rhs=codes.bitcast(FP8X4), rhs_scale=scales, start=start, stop=stop,
             )
 
-        addend, a_bank, b_bank, inner, slices, woven, h_c, h_s = {}, {}, {}, {}, {}, {}, {}, {}
+        addend, a_bank, b_bank, inner, slices, woven, h_c, h_s, part_outer = {}, {}, {}, {}, {}, {}, {}, {}, {}
 
         def step_products(i):
             u, t0 = STEPS[i]
@@ -240,19 +249,19 @@ def tile_list_pavement_upstream_horner_kernel(
             g, first, count = UNITS[u]
             outer = ring.tile([P, HALF // count, count], F32, name="outer", tag="outer")
             nc.vector.tensor_tensor(outer[:], b_bank[i][:], inner[i][:], MULT)
+            if count == PART:
+                part_outer[PART_STARTS.index(first)] = outer
+                return
             if t0 == 0:
                 slices[u] = held("slices%d" % u, [P, PACK, count], BF16)
             for k in range(HALF // count):
                 t = t0 + k
-                if u == 0:
-                    nc.gpsimd.tensor_scalar(slices[u][:, t, :], outer[:, k, :], 1.0, low_t[:, g, t : t + 1], MULT, ADD)
-                else:
-                    nc.scalar.activation(slices[u][:, t, :], outer[:, k, :], IDENT, bias=low_t[:, g, t : t + 1])
+                nc.scalar.activation(slices[u][:, t, :], outer[:, k, :], IDENT, bias=low_t[:, g, t : t + 1])
 
         def interleave(u):
             count = UNITS[u][2]
-            woven[u] = held("woven", [P, PACK * count], BF16, tag="woven%d" % (u in (1, 5)))
-            if u == len(UNITS) - 1:
+            woven[u] = held("woven", [P, PACK * count], BF16, tag="woven%d" % (u in (0, 5)))
+            if u == 5:
                 nc.scalar.copy(
                     woven[u][:].rearrange("p (c e t) -> p c t e", e=4, t=PACK), slices[u][:].rearrange("p t (c e) -> p c t e", e=4)
                 )
@@ -263,7 +272,7 @@ def tile_list_pavement_upstream_horner_kernel(
 
         def quantise_h(u):
             count = UNITS[u][2]
-            h_c[u] = held("h_c%d" % u, [P, count], U32)
+            h_c[u] = held("h_c%d" % u, [P, count], U32, tag="slices1" if u == 0 else None)
             h_s[u] = held("h_s%d" % u, [P, count], U8)
             nc.vector.quantize_mx(out=h_c[u][:].bitcast(FP8X4), scales=h_s[u][:], in_=woven[u][:])
 
@@ -284,28 +293,7 @@ def tile_list_pavement_upstream_horner_kernel(
             rows = out[per * P * half : per * P * (half + 1), first : first + count]
             nc.sync.dma_start(rows.rearrange("(c p) j -> p c j", p=P), res[:])
 
-        part_a, part_b, part_scaled, part_inner, part_outer, part_woven, part_c, part_s = {}, {}, {}, {}, {}, {}, {}, {}
-
-        def part_products(j):
-            part_a[j] = bank(A_BANKS[(len(STEPS) + j) % 2], [P, PACK, PART])
-            part_b[j] = bank(B_BANKS[(len(STEPS) + j) % 4], [P, PACK, PART])
-            for t in range(PACK):
-                product(part_b[j][:, t, :], 1, 1, t, PART_STARTS[j], PART)
-            for t in range(PACK):
-                product(part_a[j][:, t, :], 0, 1, t, PART_STARTS[j], PART)
-
-        def part_scale(j):
-            part_scaled[j] = ring.tile([P, PACK, PART], F32, name="addend", tag="addend", bufs=A_AHEAD + 2)
-            for t in range(PACK):
-                nc.scalar.activation(part_scaled[j][:, t, :], part_b[j][:, t, :], IDENT, scale=high_t[:, 1, t : t + 1])
-
-        def part_sum(j):
-            part_inner[j] = ring.tile([P, PACK, PART], F32, name="inner", tag="inner")
-            nc.vector.tensor_tensor(part_inner[j][:], part_a[j][:], part_scaled[j][:], ADD)
-
-        def part_times_b(j):
-            part_outer[j] = ring.tile([P, PACK, PART], F32, name="outer", tag="outer")
-            nc.vector.tensor_tensor(part_outer[j][:], part_b[j][:], part_inner[j][:], MULT)
+        part_woven, part_c, part_s = {}, {}, {}
 
         def part_weave(j):
             part_woven[j] = held("part_woven", [P, PART, PACK], BF16, tag="part_woven%d" % j)
@@ -324,9 +312,9 @@ def tile_list_pavement_upstream_horner_kernel(
 
         def part_out(j):
             local = slice(PART * j, PART * (j + 1))
-            acc = bank(B_BANKS[(len(STEPS) + 2 + j) % 4], [P, OUT_TILES, PART])
+            acc = bank(B_BANKS[(len(STEPS) + j) % 4], [P, OUT_TILES, PART])
             for c in range(OUT_TILES):
-                product_out(acc[:, c, :], 0, c, h_c[1][:, local], h_s[1][:, local], c == 0, False)
+                product_out(acc[:, c, :], 0, c, h_c[5][:, local], h_s[5][:, local], c == 0, False)
             for c in range(OUT_TILES):
                 product_out(acc[:, c, :], 1, c, part_c[j][:], part_s[j][:], False, c == OUT_TILES - 1)
             res = held("part_res%d" % j, [P, OUT_TILES, PART], F32)
@@ -335,52 +323,39 @@ def tile_list_pavement_upstream_horner_kernel(
             nc.sync.dma_start(columns.rearrange("(c p) j -> p c j", p=P), res[:])
 
         for i in range(A_AHEAD):
+            if i == AHEAD:
+                round_w1(1, 1, CAST_PARTS)
             step_addend(i)
             if i < AHEAD:
                 step_products(i)
-        quantise_w1(1, 0)
         step_inner(0)
         for i in range(len(STEPS)):
-            u = STEPS[i][0]
-            if i == 1:
-                round_w1(1, 1, CAST_PARTS)
-                quantise_w1(1, 1)
-            if i + 2 == len(STEPS):
-                part_scale(0)
-            if i == 2:
-                order_w2_words(1)
-                w3_w, w3_s = load_w3()
             if i + AHEAD < len(STEPS):
                 step_products(i + AHEAD)
-            elif i + AHEAD - len(STEPS) < len(PART_STARTS):
-                part_products(i + AHEAD - len(STEPS))
             if i + 1 < len(STEPS):
                 step_inner(i + 1)
             step_outer(i)
+            if i == 0:
+                quantise_w1(1, 0)
+            if i == 1:
+                quantise_w1(1, 1)
+            if i == 2:
+                order_w2_words(1)
+                w3_w = load_w3()
             if i + A_AHEAD < len(STEPS):
                 step_addend(i + A_AHEAD)
             for done in QUANTISE_AT.get(i, ()):
                 quantise_h(done)
-            if i in (3, 5):
-                interleave(u)
-            if i in (8, 10, 12):
-                interleave(i // 2 - 2)
-            if i in (11, 12):
-                unit_out(2, i - 11, OUT_BANKS)
+            for done in INTERLEAVE_AT.get(i, ()):
+                interleave(done)
+            if i in (11, 13):
+                unit_out(i // 2 - 3, 0, OUT_BANKS)
+                unit_out(i // 2 - 3, 1, OUT_BANKS)
 
-        part_scale(1)
-        interleave(5)
-        part_sum(0)
-        part_sum(1)
-        unit_out(3, 0, OUT_BANKS)
-        unit_out(3, 1, OUT_BANKS)
-        part_times_b(0)
-        part_times_b(1)
-        quantise_h(4)
-        quantise_h(5)
+        unit_out(4, 0, A_BANKS)
+        unit_out(4, 1, A_BANKS)
         part_weave(0)
-        unit_out(5, 0, A_BANKS)
-        unit_out(5, 1, A_BANKS)
+        quantise_h(5)
         part_weave(1)
         part_quantise(0)
         part_quantise(1)

@@ -26,17 +26,17 @@ QUADS = 4
 OUT_TILES = N // P
 SCALE_ROW0 = 96
 AHEAD = 3
-A_AHEAD = 5
+A_AHEAD = 4
 RING = 4
 CAST_PARTS = 4
 QUARTER = HALF // 2
-UNITS = [(0, 0, HALF), (0, HALF, QUARTER), (1, 0, QUARTER), (1, QUARTER, QUARTER), (1, HALF, QUARTER), (0, HALF + QUARTER, QUARTER)]
-PART_STARTS = list(range(HALF + QUARTER, S, PART))
-UNITS = UNITS + [(1, first, PART) for first in PART_STARTS]
-GROUP0_UNIT = {0: 0, QUARTER: 0, HALF: 1}
+UNITS = [(0, 0, HALF), (1, 0, HALF), (0, HALF, HALF), (1, HALF, QUARTER), (1, HALF + QUARTER, QUARTER)]
+LAST = len(UNITS) - 1
+GROUP0_UNIT = {0: 0, HALF: 2, HALF + QUARTER: 2}
 STEPS = [(u, t0) for u, unit in enumerate(UNITS) for t0 in range(0, PACK, HALF // unit[2])]
-INTERLEAVE_AT = {3: (0,), 5: (1,), 7: (2,), 9: (3,), 11: (4,), 13: (5,)}
-QUANTISE_AT = {7: (0, 1), 9: (2,), 11: (3,), 13: (4,)}
+INTERLEAVE_AT = {3: (0,), 7: (1,), 11: (2,), 13: (3,)}
+QUANTISE_AT = {7: (0,), 10: (1,), 14: (2,)}
+LOW_ON_GPSIMD = [(0, 0), (0, 1), (0, 2), (0, 3), (1, 1)]
 A_BANKS, B_BANKS, OUT_BANKS = (0, 1), (2, 3, 4, 5), (6, 7)
 
 
@@ -123,7 +123,7 @@ def tile_list_pavement_upstream_horner_kernel(
         def own_room(which, a, s):
             return held("v_w%d%d%d" % (which, a, s), [P, HALF], U16)[:]
 
-        w1_bf, w1_c, w1_s, w2_c, w2_s = {}, {}, {}, {}, {}
+        w1_bf, w1_codes, w1_c, w1_s, w2_c, w2_s = {}, {}, {}, {}, {}, {}
 
         def round_w1(g, a, parts):
             w1_bf[g, a] = held("w1_bf", [P, PACK * PASS], BF16, tag="w1_bf%d%d" % (g, a))
@@ -134,7 +134,7 @@ def tile_list_pavement_upstream_horner_kernel(
                 nc.scalar.copy(dst[:, ms, :, :], src[:, ms, :, :])
 
         def quantise_w1(g, a):
-            w1_c[g, a] = held("w1_c%d%d" % (g, a), [P, PASS], U32, tag="w1_raw0" if (g, a) == (1, 0) else None)
+            w1_c[g, a] = held("w1_c%d%d" % (g, a), [P, PASS], U32, tag="addend1" if (g, a) == (1, 1) else None)
             w1_s[g, a] = held("w1_s%d%d" % (g, a), [P, PASS], U8)
             nc.vector.quantize_mx(out=w1_c[g, a][:].bitcast(FP8X4), scales=w1_s[g, a][:], in_=w1_bf[g, a][:])
 
@@ -147,18 +147,11 @@ def tile_list_pavement_upstream_horner_kernel(
                 )
 
         def order_w2_words(g):
-            w2_c[g] = held("w2_c%d" % g, [P, 2, PASS], U32)
-            if g == 1:
-                nc.vector.tensor_copy(
-                    w2_c[g][:].bitcast(I32).rearrange("p a (t m) -> p a m t", t=PACK),
-                    w2_raw[g].rearrange("p a (m t) -> p a m t", t=PACK),
-                )
-                return
-            for t in range(PACK):
-                nc.gpsimd.tensor_copy(
-                    w2_c[g][:].bitcast(I32).rearrange("p a (t m) -> p a t m", t=PACK)[:, :, t, :],
-                    w2_raw[g].rearrange("p a (m t) -> p a t m", t=PACK)[:, :, t, :],
-                )
+            w2_c[g] = held("w2_c%d" % g, [P, 2, PASS], U32, tag="addend2" if g == 1 else None)
+            nc.vector.tensor_copy(
+                w2_c[g][:].bitcast(I32).rearrange("p a (t m) -> p a m t", t=PACK),
+                w2_raw[g].rearrange("p a (m t) -> p a m t", t=PACK),
+            )
 
         def second_half_words(wanted, tag):
             late = held("late", [P, len(wanted), HALF], U16, tag=tag)
@@ -168,6 +161,7 @@ def tile_list_pavement_upstream_horner_kernel(
         round_w1(0, 0, 1)
         load_w2(0, held("w2_raw", [P, 2, PASS], I32, tag="w1_raw0")[:])
         round_w1(0, 1, 1)
+        load_w1(1, 1, w1_room("w1_raw1"))
         round_w1(1, 0, 1)
         for a in range(2):
             for which in range(2):
@@ -178,9 +172,7 @@ def tile_list_pavement_upstream_horner_kernel(
         order_w2_scales(1)
         quantise_w1(0, 0)
         quantise_w1(0, 1)
-        order_w2_words(0)
-        third = held("third", [P, PACK * PASS + 24], F32, tag="w1_raw1")
-        per_row = third[:, PACK * PASS :].rearrange("p (v c) -> p v c", c=8)
+        per_row = held("per_row", [P, 3, 8], F32, tag="picked_s")
         high_t = per_row[:, 0, :].rearrange("p (g t) -> p g t", g=2)
         low_t = per_row[:, 1, :].rearrange("p (g t) -> p g t", g=2)
         bias_t = per_row[:, 2, 0:OUT_TILES]
@@ -188,9 +180,11 @@ def tile_list_pavement_upstream_horner_kernel(
         nc.sync.dma_start(low_t, low.rearrange("(g p t) -> p g t", g=2, t=PACK))
         with nc.allow_non_contiguous_dma("the bias has one value for each partition of an output tile"):
             nc.sync.dma_start(bias_t, bias.rearrange("(c p) -> p c", p=P))
-        load_w1(1, 1, third[:, 0 : PACK * PASS].rearrange("p (i c) -> p i c", i=PACK))
         load_w2(1, held("w2_raw", [P, 2, PASS], I32, tag="tab_s")[:])
-        second_half_words([(0, 1), (1, 1)], "w1_bf01")
+        second_half_words([(0, 1)], "w1_bf01")
+        order_w2_words(0)
+        quantise_w1(1, 0)
+        second_half_words([(1, 1)], "w1_raw0")
 
         def load_w3():
             words = held("w3_w", [P, 2, N], U16, tag="tab_s")
@@ -230,10 +224,14 @@ def tile_list_pavement_upstream_horner_kernel(
         def step_addend(i):
             u, t0 = STEPS[i]
             g, first, count = UNITS[u]
-            a_bank[i] = bank(A_BANKS[i % 2], [P, HALF // count, count])
+            shape = [P, HALF // count, count]
+            a_bank[i] = bank(A_BANKS[i % 2], shape)
             for k in range(HALF // count):
                 product(a_bank[i][:, k, :], 0, g, t0 + k, first, count)
-            addend[i] = ring.tile([P, HALF // count, count], F32, name="addend", tag="addend", bufs=A_AHEAD + 2)
+            if i in (1, 2, 8):
+                addend[i] = held("addend%d" % i, shape, F32)
+            else:
+                addend[i] = ring.tile(shape, F32, name="addend", tag="addend", bufs=A_AHEAD + 2)
             nc.scalar.copy(addend[i][:], a_bank[i][:])
 
         def step_inner(i):
@@ -247,21 +245,33 @@ def tile_list_pavement_upstream_horner_kernel(
         def step_outer(i):
             u, t0 = STEPS[i]
             g, first, count = UNITS[u]
-            outer = ring.tile([P, HALF // count, count], F32, name="outer", tag="outer")
-            nc.vector.tensor_tensor(outer[:], b_bank[i][:], inner[i][:], MULT)
-            if count == PART:
-                part_outer[PART_STARTS.index(first)] = outer
+            width = HALF // count
+            if u == LAST:
+                if t0 == 0:
+                    slices[u] = held("last_outer", [P, PACK, count], F32)
+                nc.vector.tensor_tensor(slices[u][:, t0 : t0 + width, :], b_bank[i][:], inner[i][:], MULT)
                 return
+            outer = ring.tile([P, width, count], F32, name="outer", tag="outer")
+            nc.vector.tensor_tensor(outer[:], b_bank[i][:], inner[i][:], MULT)
             if t0 == 0:
                 slices[u] = held("slices%d" % u, [P, PACK, count], BF16)
-            for k in range(HALF // count):
+            for k in range(width):
                 t = t0 + k
-                nc.scalar.activation(slices[u][:, t, :], outer[:, k, :], IDENT, bias=low_t[:, g, t : t + 1])
+                if (u, t) in LOW_ON_GPSIMD:
+                    nc.gpsimd.tensor_scalar(slices[u][:, t, :], outer[:, k, :], 1.0, low_t[:, g, t : t + 1], MULT, ADD)
+                else:
+                    nc.scalar.activation(slices[u][:, t, :], outer[:, k, :], IDENT, bias=low_t[:, g, t : t + 1])
 
         def interleave(u):
-            count = UNITS[u][2]
-            woven[u] = held("woven", [P, PACK * count], BF16, tag="woven%d" % (u in (0, 5)))
-            if u == 5:
+            g, first, count = UNITS[u]
+            woven[u] = held("woven", [P, PACK * count], BF16, tag="woven%d" % (u if u != 2 else 0))
+            if u == LAST:
+                nc.vector.tensor_tensor(
+                    woven[u][:].rearrange("p (c e t) -> p c t e", e=4, t=PACK),
+                    slices[u][:].rearrange("p t (c e) -> p c t e", e=4),
+                    low_t[:, g, :].unsqueeze(1).unsqueeze(3).to_broadcast([P, count // 4, PACK, 4]), ADD,
+                )
+            elif u == LAST - 1:
                 nc.scalar.copy(
                     woven[u][:].rearrange("p (c e t) -> p c t e", e=4, t=PACK), slices[u][:].rearrange("p t (c e) -> p c t e", e=4)
                 )
@@ -272,7 +282,7 @@ def tile_list_pavement_upstream_horner_kernel(
 
         def quantise_h(u):
             count = UNITS[u][2]
-            h_c[u] = held("h_c%d" % u, [P, count], U32, tag="slices1" if u == 0 else None)
+            h_c[u] = held("h_c%d" % u, [P, count], U32, tag="addend8" if u == 0 else None)
             h_s[u] = held("h_s%d" % u, [P, count], U8)
             nc.vector.quantize_mx(out=h_c[u][:].bitcast(FP8X4), scales=h_s[u][:], in_=woven[u][:])
 
@@ -287,60 +297,34 @@ def tile_list_pavement_upstream_horner_kernel(
                 product_out(acc[:, e, :], 0, per * half + e, h_c[base][:, tokens], h_s[base][:, tokens], e == 0, False)
             for e in range(per):
                 product_out(acc[:, e, :], 1, per * half + e, h_c[u][:], h_s[u][:], False, e == per - 1)
-            for e in range(per):
-                c = per * half + e
-                nc.scalar.activation(res[:, e, :], acc[:, e, :], IDENT, bias=bias_t[:, c : c + 1])
+            if u == LAST:
+                per_tile = bias_t[:, per * half : per * (half + 1)].unsqueeze(2).to_broadcast([P, per, count])
+                nc.vector.tensor_tensor(res[:], acc[:], per_tile, ADD)
+            else:
+                for e in range(per):
+                    c = per * half + e
+                    nc.scalar.activation(res[:, e, :], acc[:, e, :], IDENT, bias=bias_t[:, c : c + 1])
             rows = out[per * P * half : per * P * (half + 1), first : first + count]
             nc.sync.dma_start(rows.rearrange("(c p) j -> p c j", p=P), res[:])
 
-        part_woven, part_c, part_s = {}, {}, {}
-
-        def part_weave(j):
-            part_woven[j] = held("part_woven", [P, PART, PACK], BF16, tag="part_woven%d" % j)
-            nc.vector.tensor_tensor(
-                part_woven[j][:].rearrange("p (c e) t -> p c t e", e=4),
-                part_outer[j][:].rearrange("p t (c e) -> p c t e", e=4),
-                low_t[:, 1, :].unsqueeze(1).unsqueeze(3).to_broadcast([P, PART // 4, PACK, 4]), ADD,
-            )
-
-        def part_quantise(j):
-            part_c[j] = held("part_c%d" % j, [P, PART], U32)
-            part_s[j] = held("part_s%d" % j, [P, PART], U8)
-            nc.vector.quantize_mx(
-                out=part_c[j][:].bitcast(FP8X4), scales=part_s[j][:], in_=part_woven[j][:].rearrange("p c t -> p (c t)")
-            )
-
-        def part_out(j):
-            local = slice(PART * j, PART * (j + 1))
-            acc = bank(B_BANKS[(len(STEPS) + j) % 4], [P, OUT_TILES, PART])
-            for c in range(OUT_TILES):
-                product_out(acc[:, c, :], 0, c, h_c[5][:, local], h_s[5][:, local], c == 0, False)
-            for c in range(OUT_TILES):
-                product_out(acc[:, c, :], 1, c, part_c[j][:], part_s[j][:], False, c == OUT_TILES - 1)
-            res = held("part_res%d" % j, [P, OUT_TILES, PART], F32)
-            nc.vector.tensor_tensor(res[:], acc[:], bias_t.unsqueeze(2).to_broadcast([P, OUT_TILES, PART]), ADD)
-            columns = out[:, PART_STARTS[j] : PART_STARTS[j] + PART]
-            nc.sync.dma_start(columns.rearrange("(c p) j -> p c j", p=P), res[:])
-
         for i in range(A_AHEAD):
-            if i == AHEAD:
-                round_w1(1, 1, CAST_PARTS)
+            if i == 2:
+                round_w1(1, 1, 1)
             step_addend(i)
             if i < AHEAD:
                 step_products(i)
         step_inner(0)
         for i in range(len(STEPS)):
-            if i + AHEAD < len(STEPS):
+            if i + AHEAD < len(STEPS) and i != 1:
                 step_products(i + AHEAD)
             if i + 1 < len(STEPS):
                 step_inner(i + 1)
             step_outer(i)
             if i == 0:
-                quantise_w1(1, 0)
-            if i == 1:
                 quantise_w1(1, 1)
-            if i == 2:
+            if i == 1:
                 order_w2_words(1)
+                step_products(4)
                 w3_w = load_w3()
             if i + A_AHEAD < len(STEPS):
                 step_addend(i + A_AHEAD)
@@ -348,16 +332,13 @@ def tile_list_pavement_upstream_horner_kernel(
                 quantise_h(done)
             for done in INTERLEAVE_AT.get(i, ()):
                 interleave(done)
-            if i in (11, 13):
-                unit_out(i // 2 - 3, 0, OUT_BANKS)
-                unit_out(i // 2 - 3, 1, OUT_BANKS)
+            if 11 <= i < 15:
+                unit_out(1, i - 11, OUT_BANKS)
 
-        unit_out(4, 0, A_BANKS)
-        unit_out(4, 1, A_BANKS)
-        part_weave(0)
-        quantise_h(5)
-        part_weave(1)
-        part_quantise(0)
-        part_quantise(1)
-        part_out(0)
-        part_out(1)
+        interleave(LAST)
+        quantise_h(3)
+        quantise_h(LAST)
+        unit_out(3, 0, A_BANKS)
+        unit_out(3, 1, A_BANKS)
+        unit_out(LAST, 0, B_BANKS)
+        unit_out(LAST, 1, B_BANKS)

@@ -30,12 +30,12 @@ A_AHEAD = 4
 RING = 4
 CAST_PARTS = 4
 QUARTER = HALF // 2
-UNITS = [(0, 0, HALF), (1, 0, HALF), (0, HALF, HALF), (1, HALF, QUARTER), (1, HALF + QUARTER, QUARTER)]
+UNITS = [(0, 0, HALF), (0, HALF, HALF), ] + [(1, first, QUARTER) for first in range(0, S, QUARTER)]
 LAST = len(UNITS) - 1
-GROUP0_UNIT = {0: 0, HALF: 2, HALF + QUARTER: 2}
+GROUP0_UNIT = {0: 0, QUARTER: 0, HALF: 1, HALF + QUARTER: 1}
 STEPS = [(u, t0) for u, unit in enumerate(UNITS) for t0 in range(0, PACK, HALF // unit[2])]
-INTERLEAVE_AT = {3: (0,), 7: (1,), 11: (2,), 13: (3,)}
-QUANTISE_AT = {7: (0,), 10: (1,), 14: (2,)}
+INTERLEAVE_AT = {3: (0,), 7: (1,), 10: (2,), 12: (3,), 14: (4,)}
+QUANTISE_AT = {7: (0,), 10: (1,), 12: (2,), 14: (3,), 15: (4,)}
 LOW_ON_GPSIMD = [(0, 0), (0, 1), (0, 2), (0, 3), (1, 1)]
 A_BANKS, B_BANKS, OUT_BANKS = (0, 1), (2, 3, 4, 5), (6, 7)
 
@@ -134,7 +134,7 @@ def tile_list_pavement_upstream_horner_kernel(
                 nc.scalar.copy(dst[:, ms, :, :], src[:, ms, :, :])
 
         def quantise_w1(g, a):
-            w1_c[g, a] = held("w1_c%d%d" % (g, a), [P, PASS], U32, tag="addend1" if (g, a) == (1, 1) else None)
+            w1_c[g, a] = held("w1_c%d%d" % (g, a), [P, PASS], U32, tag="addend3" if (g, a) == (1, 1) else None)
             w1_s[g, a] = held("w1_s%d%d" % (g, a), [P, PASS], U8)
             nc.vector.quantize_mx(out=w1_c[g, a][:].bitcast(FP8X4), scales=w1_s[g, a][:], in_=w1_bf[g, a][:])
 
@@ -147,7 +147,7 @@ def tile_list_pavement_upstream_horner_kernel(
                 )
 
         def order_w2_words(g):
-            w2_c[g] = held("w2_c%d" % g, [P, 2, PASS], U32, tag="addend2" if g == 1 else None)
+            w2_c[g] = held("w2_c%d" % g, [P, 2, PASS], U32, tag="addend4" if g == 1 else None)
             nc.vector.tensor_copy(
                 w2_c[g][:].bitcast(I32).rearrange("p a (t m) -> p a m t", t=PACK),
                 w2_raw[g].rearrange("p a (m t) -> p a m t", t=PACK),
@@ -228,7 +228,7 @@ def tile_list_pavement_upstream_horner_kernel(
             a_bank[i] = bank(A_BANKS[i % 2], shape)
             for k in range(HALF // count):
                 product(a_bank[i][:, k, :], 0, g, t0 + k, first, count)
-            if i in (1, 2, 8):
+            if i in (3, 4, 8):
                 addend[i] = held("addend%d" % i, shape, F32)
             else:
                 addend[i] = ring.tile(shape, F32, name="addend", tag="addend", bufs=A_AHEAD + 2)
@@ -246,9 +246,9 @@ def tile_list_pavement_upstream_horner_kernel(
             u, t0 = STEPS[i]
             g, first, count = UNITS[u]
             width = HALF // count
-            if u == LAST:
+            if u >= LAST - 1:
                 if t0 == 0:
-                    slices[u] = held("last_outer", [P, PACK, count], F32)
+                    slices[u] = held("outer%d" % u, [P, PACK, count], F32)
                 nc.vector.tensor_tensor(slices[u][:, t0 : t0 + width, :], b_bank[i][:], inner[i][:], MULT)
                 return
             outer = ring.tile([P, width, count], F32, name="outer", tag="outer")
@@ -264,16 +264,12 @@ def tile_list_pavement_upstream_horner_kernel(
 
         def interleave(u):
             g, first, count = UNITS[u]
-            woven[u] = held("woven", [P, PACK * count], BF16, tag="woven%d" % (u if u != 2 else 0))
-            if u == LAST:
+            woven[u] = held("woven", [P, PACK * count], BF16, tag={2: "woven1", 3: "woven1", 4: "slices3"}.get(u, "woven%d" % u))
+            if u >= LAST - 1:
                 nc.vector.tensor_tensor(
                     woven[u][:].rearrange("p (c e t) -> p c t e", e=4, t=PACK),
                     slices[u][:].rearrange("p t (c e) -> p c t e", e=4),
                     low_t[:, g, :].unsqueeze(1).unsqueeze(3).to_broadcast([P, count // 4, PACK, 4]), ADD,
-                )
-            elif u == LAST - 1:
-                nc.scalar.copy(
-                    woven[u][:].rearrange("p (c e t) -> p c t e", e=4, t=PACK), slices[u][:].rearrange("p t (c e) -> p c t e", e=4)
                 )
             else:
                 nc.gpsimd.tensor_scalar(
@@ -282,7 +278,7 @@ def tile_list_pavement_upstream_horner_kernel(
 
         def quantise_h(u):
             count = UNITS[u][2]
-            h_c[u] = held("h_c%d" % u, [P, count], U32, tag="addend8" if u == 0 else None)
+            h_c[u] = held("h_c%d" % u, [P, count], U32, tag={0: "addend8"}.get(u))
             h_s[u] = held("h_s%d" % u, [P, count], U8)
             nc.vector.quantize_mx(out=h_c[u][:].bitcast(FP8X4), scales=h_s[u][:], in_=woven[u][:])
 
@@ -308,23 +304,21 @@ def tile_list_pavement_upstream_horner_kernel(
             nc.sync.dma_start(rows.rearrange("(c p) j -> p c j", p=P), res[:])
 
         for i in range(A_AHEAD):
-            if i == 2:
-                round_w1(1, 1, 1)
             step_addend(i)
             if i < AHEAD:
                 step_products(i)
+        round_w1(1, 1, 2)
         step_inner(0)
         for i in range(len(STEPS)):
-            if i + AHEAD < len(STEPS) and i != 1:
+            if i + AHEAD < len(STEPS):
                 step_products(i + AHEAD)
             if i + 1 < len(STEPS):
                 step_inner(i + 1)
             step_outer(i)
-            if i == 0:
+            if i == 2:
                 quantise_w1(1, 1)
-            if i == 1:
+            if i == 3:
                 order_w2_words(1)
-                step_products(4)
                 w3_w = load_w3()
             if i + A_AHEAD < len(STEPS):
                 step_addend(i + A_AHEAD)
@@ -332,13 +326,13 @@ def tile_list_pavement_upstream_horner_kernel(
                 quantise_h(done)
             for done in INTERLEAVE_AT.get(i, ()):
                 interleave(done)
-            if 11 <= i < 15:
-                unit_out(1, i - 11, OUT_BANKS)
+            if i in (13, 15):
+                unit_out(i // 2 - 4, 0, OUT_BANKS)
+                unit_out(i // 2 - 4, 1, OUT_BANKS)
 
         interleave(LAST)
-        quantise_h(3)
         quantise_h(LAST)
-        unit_out(3, 0, A_BANKS)
-        unit_out(3, 1, A_BANKS)
+        unit_out(4, 0, A_BANKS)
+        unit_out(4, 1, A_BANKS)
         unit_out(LAST, 0, B_BANKS)
         unit_out(LAST, 1, B_BANKS)

@@ -50,7 +50,7 @@ def tile_list_pavement_upstream_horner_kernel(
         psum = ctx.enter_context(tc.psum_pool(name="psum", bufs=1))
 
         def held(name, shape, dtype, tag=None):
-            return keep.tile(shape, dtype, name=name, tag=tag or name, align_bytes=64)
+            return keep.tile(shape, dtype, name=name, tag=tag or name, align_bytes=256)
 
         def bank(index, shape):
             return psum.tile(shape, F32, name="bank", tag="bank%d" % index)
@@ -163,11 +163,13 @@ def tile_list_pavement_upstream_horner_kernel(
         round_w1(0, 1, 1)
         load_w1(1, 1, w1_room("w1_raw1"))
         round_w1(1, 0, 1)
-        for a in range(2):
-            for which in range(2):
-                gather_words(which, a, 0, own_room(which, a, 0))
         for which in range(2):
-            gather_words(which, 0, 1, own_room(which, 0, 1))
+            whole = held("v_w%d0" % which, [P, S], U16)
+            nc.vector.tensor_copy(whole[:], tab_w[0][:].indirect(lists[which][:]))
+            for s in range(2):
+                v_w[which, 0, s] = whole[:, HALF * s : HALF * (s + 1)]
+        for which in range(2):
+            gather_words(which, 1, 0, own_room(which, 1, 0))
         order_w2_scales(0)
         order_w2_scales(1)
         quantise_w1(0, 0)

@@ -64,8 +64,8 @@ def tile_list_pavement_upstream_horner_kernel(
         w2_s_raw = held("w2_s_raw", [P, 2, H], U8)
         nc.gpsimd.memset(w2_s_raw[:].rearrange("p a c -> p (a c)").bitcast(I32), 0)
         tab_s = held("tab_s", [P, T], U8)
-        nc.sync.dma_start(lists[0][:], offs)
         nc.sync.dma_start(tab_s[SCALE_ROW0:P, :].bitcast(I32), tab_scales.rearrange("a q t -> (a q) t").bitcast(I32))
+        nc.sync.dma_start(lists[0][:], offs)
         nc.sync.dma_start(lists[1][:], offs2)
         load_scale_rows(w2_s_raw, w2_scales)
         w3_s = held("w3_s", [P, 2, N], U8)
@@ -189,7 +189,7 @@ def tile_list_pavement_upstream_horner_kernel(
         second_half_words([(1, 1)], "w1_raw0")
 
         def load_w3():
-            words = held("w3_w", [P, 2, N], U16, tag="tab_s")
+            words = held("w3_w", [P, 2, N], U16, tag="w1_raw1")
             nc.sync.dma_start(words[:].bitcast(I32), w3_words.rearrange("a p b -> p a b").bitcast(I32))
             return words
 
@@ -233,13 +233,13 @@ def tile_list_pavement_upstream_horner_kernel(
             if i in (3, 4, 8):
                 addend[i] = held("addend%d" % i, shape, F32)
             else:
-                addend[i] = ring.tile(shape, F32, name="addend", tag="addend", bufs=A_AHEAD + 2)
+                addend[i] = ring.tile(shape, F32, name="addend", tag="addend", align_bytes=256, bufs=A_AHEAD + 2)
             nc.scalar.copy(addend[i][:], a_bank[i][:])
 
         def step_inner(i):
             u, t0 = STEPS[i]
             g, first, count = UNITS[u]
-            inner[i] = ring.tile([P, HALF // count, count], F32, name="inner", tag="inner")
+            inner[i] = ring.tile([P, HALF // count, count], F32, name="inner", tag="inner", align_bytes=256)
             for k in range(HALF // count):
                 per_row = high_t[:, g, t0 + k : t0 + k + 1]
                 nc.vector.scalar_tensor_tensor(inner[i][:, k, :], b_bank[i][:, k, :], per_row, addend[i][:, k, :], MULT, ADD)
@@ -253,7 +253,7 @@ def tile_list_pavement_upstream_horner_kernel(
                     slices[u] = held("outer%d" % u, [P, PACK, count], F32)
                 nc.vector.tensor_tensor(slices[u][:, t0 : t0 + width, :], b_bank[i][:], inner[i][:], MULT)
                 return
-            outer = ring.tile([P, width, count], F32, name="outer", tag="outer")
+            outer = ring.tile([P, width, count], F32, name="outer", tag="outer", align_bytes=256)
             nc.vector.tensor_tensor(outer[:], b_bank[i][:], inner[i][:], MULT)
             if t0 == 0:
                 slices[u] = held("slices%d" % u, [P, PACK, count], BF16)
@@ -266,7 +266,7 @@ def tile_list_pavement_upstream_horner_kernel(
 
         def interleave(u):
             g, first, count = UNITS[u]
-            woven[u] = held("woven", [P, PACK * count], BF16, tag={2: "woven1", 3: "woven1", 4: "slices3"}.get(u, "woven%d" % u))
+            woven[u] = held("woven", [P, PACK * count], BF16, tag={2: "woven1", 3: "woven1", 0: "tab_s", 4: "slices3"}.get(u, "woven%d" % u))
             if u >= LAST - 1:
                 nc.vector.tensor_tensor(
                     woven[u][:].rearrange("p (c e t) -> p c t e", e=4, t=PACK),

@@ -295,7 +295,7 @@ def tile_list_pavement_upstream_horner_kernel(
                 product_out(acc[:, e, :], 0, per * half + e, h_c[base][:, tokens], h_s[base][:, tokens], e == 0, False)
             for e in range(per):
                 product_out(acc[:, e, :], 1, per * half + e, h_c[u][:], h_s[u][:], False, e == per - 1)
-            if u == LAST:
+            if u == LAST and half == 0:
                 per_tile = bias_t[:, per * half : per * (half + 1)].unsqueeze(2).to_broadcast([P, per, count])
                 nc.vector.tensor_tensor(res[:], acc[:], per_tile, ADD)
             else:
@@ -336,5 +336,5 @@ def tile_list_pavement_upstream_horner_kernel(
         quantise_h(LAST)
         unit_out(4, 0, A_BANKS)
         unit_out(4, 1, A_BANKS)
-        unit_out(LAST, 0, B_BANKS)
-        unit_out(LAST, 1, B_BANKS)
+        unit_out(LAST, 0, B_BANKS[2:])
+        unit_out(LAST, 1, B_BANKS[2:])

from contextlib import ExitStack

import concourse.mybir as mybir

K, T, S, H, N = 1024, 4096, 1024, 1024, 512
FLOPS = 2 * (2 * K * H * S + H * N * S)

F32 = mybir.dt.float32
BF16 = mybir.dt.bfloat16
I32 = mybir.dt.int32
U32 = mybir.dt.uint32
U16 = mybir.dt.uint16
U8 = mybir.dt.uint8
FP8X4 = mybir.dt.float8_e4m3fn_x4
FP4X4 = mybir.dt.float4_e2m1fn_x4
MULT = mybir.AluOpType.mult
ADD = mybir.AluOpType.add
IDENT = mybir.ActivationFunctionType.Identity

P = 128
PACK = 4
PASS = P * PACK
HALF = 512
PART = 128
QUADS = 4
OUT_TILES = N // P
SCALE_ROW0 = 96
AHEAD = 3
A_AHEAD = 4
RING = 4
CAST_PARTS = 4
QUARTER = HALF // 2
UNITS = [(0, 0, HALF), (0, HALF, HALF), ] + [(1, first, QUARTER) for first in range(0, S, QUARTER)]
LAST = len(UNITS) - 1
GROUP0_UNIT = {0: 0, QUARTER: 0, HALF: 1, HALF + QUARTER: 1}
STEPS = [(u, t0) for u, unit in enumerate(UNITS) for t0 in range(0, PACK, HALF // unit[2])]
INTERLEAVE_AT = {3: (0,), 7: (1,), 10: (2,), 12: (3,), 14: (4,)}
QUANTISE_AT = {7: (0,), 10: (1,), 12: (2,), 14: (3,), 15: (4,)}
LOW_ON_GPSIMD = [(0, 0), (0, 1), (0, 2), (0, 3), (1, 1)]
A_BANKS, B_BANKS, OUT_BANKS = (0, 1), (2, 3, 4, 5), (6, 7)


def tile_list_pavement_upstream_horner_kernel(
    tc, tab_words, tab_scales, offs, offs2, w1, w2_words, w2_scales, low, high, w3_words, w3_scales, bias, out
):
    nc = tc.nc
    with ExitStack() as ctx:
        keep = ctx.enter_context(tc.tile_pool(name="keep", bufs=1))
        ring = ctx.enter_context(tc.tile_pool(name="ring", bufs=RING))
        psum = ctx.enter_context(tc.psum_pool(name="psum", bufs=1))

        def held(name, shape, dtype, tag=None):
            return keep.tile(shape, dtype, name=name, tag=tag or name, align_bytes=256)

        def bank(index, shape):
            return psum.tile(shape, F32, name="bank", tag="bank%d" % index)

        def load_scale_rows(tile, scales):
            for q in range(QUADS):
                rows = scales[:, 4 * q : 4 * q + 4, :].rearrange("a r c -> r a c")
                nc.sync.dma_start(tile[32 * q : 32 * q + 4, :, :].bitcast(I32), rows.bitcast(I32))

        lists = [held("list_a", [P, S // 16], U16), held("list_b", [P, S // 16], U16)]
        w2_s_raw = held("w2_s_raw", [P, 2, H], U8)
        nc.gpsimd.memset(w2_s_raw[:].rearrange("p a c -> p (a c)").bitcast(I32), 0)
        tab_s = held("tab_s", [P, T], U8)
        nc.sync.dma_start(tab_s[SCALE_ROW0:P, :].bitcast(I32), tab_scales.rearrange("a q t -> (a q) t").bitcast(I32))
        nc.sync.dma_start(lists[0][:], offs)
        nc.sync.dma_start(lists[1][:], offs2)
        load_scale_rows(w2_s_raw, w2_scales)
        w3_s = held("w3_s", [P, 2, N], U8)
        nc.gpsimd.memset(w3_s[:].rearrange("p a c -> p (a c)").bitcast(I32), 0)
        nc.vector.memset(tab_s[0:SCALE_ROW0, :].bitcast(I32), 0)
        v_s_all = held("v_s_all", [P, 4 * S], U8)
        nc.gpsimd.memset(v_s_all[:].bitcast(I32), 0)
        v_s = [v_s_all[:, 2 * S * a : 2 * S * (a + 1)] for a in range(2)]

        tab_w = [held("tab_w%d" % a, [P, T], U16) for a in range(2)]
        w1_raw, w2_raw = {}, {}

        def load_tab(a):
            nc.sync.dma_start(tab_w[a][:].bitcast(I32), tab_words[a].bitcast(I32))

        def load_w1(g, a, room):
            w1_raw[g, a] = room
            rows = w1[PASS * a : PASS * (a + 1), PASS * g : PASS * (g + 1)]
            nc.sync.dma_start(room, rows.rearrange("(p i) c -> p i c", i=PACK))

        def w1_room(tag):
            return held("w1_raw", [P, PACK, PASS], F32, tag=tag)[:]

        def load_w2(g, room):
            w2_raw[g] = room
            words = w2_words.rearrange("a p c i -> p a (c i)")[:, :, PACK * PASS * g : PACK * PASS * (g + 1)]
            nc.sync.dma_start(room, words.bitcast(I32))

        load_tab(0)
        load_scale_rows(w3_s, w3_scales)
        load_w1(0, 0, w1_room("w1_raw0"))
        load_tab(1)
        load_w1(0, 1, w1_room("w1_raw1"))

        picked_s = held("picked_s", [P, 2 * S], U8)
        for which in range(2):
            nc.vector.tensor_copy(picked_s[:, S * which : S * (which + 1)], tab_s[:].indirect(lists[which][:]))

        def move_scale_rows(a):
            for q in range(QUADS):
                row = SCALE_ROW0 + 16 * a + 4 * q
                nc.sync.dma_start(v_s[a][32 * q : 32 * q + 4, :].bitcast(I32), picked_s[row : row + 4, :].bitcast(I32))

        move_scale_rows(0)
        load_w1(1, 0, w1_room("tab_s"))
        move_scale_rows(1)

        v_w = {}

        def gather_words(which, a, s, room):
            v_w[which, a, s] = room
            entries = slice(HALF // 16 * s, HALF // 16 * (s + 1))
            nc.vector.tensor_copy(room, tab_w[a][:].indirect(lists[which][:, entries]))

        def own_room(which, a, s):
            return held("v_w%d%d%d" % (which, a, s), [P, HALF], U16)[:]

        w1_bf, w1_codes, w1_c, w1_s, w2_c, w2_s = {}, {}, {}, {}, {}, {}

        def round_w1(g, a, parts):
            w1_bf[g, a] = held("w1_bf", [P, PACK * PASS], BF16, tag="w1_bf%d%d" % (g, a))
            dst = w1_bf[g, a][:].rearrange("p (t m i) -> p m i t", t=PACK, i=PACK)
            src = w1_raw[g, a].rearrange("p i (m t) -> p m i t", t=PACK)
            for part in range(parts):
                ms = slice(P // parts * part, P // parts * (part + 1))
                nc.scalar.copy(dst[:, ms, :, :], src[:, ms, :, :])

        def quantise_w1(g, a):
            w1_c[g, a] = held("w1_c%d%d" % (g, a), [P, PASS], U32, tag="addend3" if (g, a) == (1, 1) else None)
            w1_s[g, a] = held("w1_s%d%d" % (g, a), [P, PASS], U8)
            nc.vector.quantize_mx(out=w1_c[g, a][:].bitcast(FP8X4), scales=w1_s[g, a][:], in_=w1_bf[g, a][:])

        def order_w2_scales(g):
            w2_s[g] = held("w2_s%d" % g, [P, 2, PASS], U8)
            for a in range(2):
                nc.gpsimd.tensor_copy(
                    w2_s[g][:, a, :].rearrange("p (t m) -> p t m", t=PACK),
                    w2_s_raw[:, a, PASS * g : PASS * (g + 1)].rearrange("p (m t) -> p t m", t=PACK),
                )

        def order_w2_words(g):
            w2_c[g] = held("w2_c%d" % g, [P, 2, PASS], U32, tag="addend4" if g == 1 else None)
            nc.vector.tensor_copy(
                w2_c[g][:].bitcast(I32).rearrange("p a (t m) -> p a m t", t=PACK),
                w2_raw[g].rearrange("p a (m t) -> p a m t", t=PACK),
            )

        def second_half_words(wanted, tag):
            late = held("late", [P, len(wanted), HALF], U16, tag=tag)
            for place, (which, a) in enumerate(wanted):
                gather_words(which, a, 1, late[:, place, :])

        round_w1(0, 0, 1)
        load_w2(0, held("w2_raw", [P, 2, PASS], I32, tag="w1_raw0")[:])
        round_w1(0, 1, 1)
        load_w1(1, 1, w1_room("w1_raw1"))
        round_w1(1, 0, 1)
        for which in range(2):
            whole = held("v_w%d0" % which, [P, S], U16)
            nc.vector.tensor_copy(whole[:], tab_w[0][:].indirect(lists[which][:]))
            for s in range(2):
                v_w[which, 0, s] = whole[:, HALF * s : HALF * (s + 1)]
        for which in range(2):
            gather_words(which, 1, 0, own_room(which, 1, 0))
        order_w2_scales(0)
        order_w2_scales(1)
        quantise_w1(0, 0)
        quantise_w1(0, 1)
        per_row = held("per_row", [P, 3, 8], F32, tag="picked_s")
        high_t = per_row[:, 0, :].rearrange("p (g t) -> p g t", g=2)
        low_t = per_row[:, 1, :].rearrange("p (g t) -> p g t", g=2)
        bias_t = per_row[:, 2, 0:OUT_TILES]
        nc.sync.dma_start(high_t, high.rearrange("(g p t) -> p g t", g=2, t=PACK))
        nc.sync.dma_start(low_t, low.rearrange("(g p t) -> p g t", g=2, t=PACK))
        with nc.allow_non_contiguous_dma("the bias has one value for each partition of an output tile"):
            nc.sync.dma_start(bias_t, bias.rearrange("(c p) -> p c", p=P))
        load_w2(1, held("w2_raw", [P, 2, PASS], I32, tag="tab_s")[:])
        second_half_words([(0, 1)], "w1_bf01")
        order_w2_words(0)
        quantise_w1(1, 0)
        second_half_words([(1, 1)], "w1_raw0")

        def load_w3():
            words = held("w3_w", [P, 2, N], U16, tag="w1_raw1")
            nc.sync.dma_start(words[:].bitcast(I32), w3_words.rearrange("a p b -> p a b").bitcast(I32))
            return words

        def product(acc, which, g, t, first, count):
            cols = slice(P * t, P * (t + 1))
            s, local = divmod(first, HALF)
            for a in range(2):
                codes = w1_c[g, a][:, cols] if which == 0 else w2_c[g][:, a, cols]
                scales = w1_s[g, a][:, cols] if which == 0 else w2_s[g][:, a, cols]
                nc.tensor.matmul_mx(
                    out=acc, lhsT=codes.bitcast(FP8X4), lhsT_scale=scales,
                    rhs=v_w[which, a, s][:, local : local + count].bitcast(FP4X4),
                    rhs_scale=v_s[a][:, S * which + first : S * which + first + count],
                    start=(a == 0), stop=(a == 1),
                )

        def product_out(acc, g, c, codes, scales, start, stop):
            cols = slice(P * c, P * (c + 1))
            nc.tensor.matmul_mx(
                out=acc, lhsT=w3_w[:, g, cols].bitcast(FP4X4), lhsT_scale=w3_s[:, g, cols],
                rhs=codes.bitcast(FP8X4), rhs_scale=scales, start=start, stop=stop,
            )

        addend, a_bank, b_bank, inner, slices, woven, h_c, h_s, part_outer = {}, {}, {}, {}, {}, {}, {}, {}, {}

        def step_products(i):
            u, t0 = STEPS[i]
            g, first, count = UNITS[u]
            shape = [P, HALF // count, count]
            b_bank[i] = bank(B_BANKS[i % 4], shape)
            for k in range(shape[1]):
                product(b_bank[i][:, k, :], 1, g, t0 + k, first, count)

        def step_addend(i):
            u, t0 = STEPS[i]
            g, first, count = UNITS[u]
            shape = [P, HALF // count, count]
            a_bank[i] = bank(A_BANKS[i % 2], shape)
            for k in range(HALF // count):
                product(a_bank[i][:, k, :], 0, g, t0 + k, first, count)
            if i in (3, 4, 8):
                addend[i] = held("addend%d" % i, shape, F32)
            else:
                addend[i] = ring.tile(shape, F32, name="addend", tag="addend", align_bytes=256, bufs=A_AHEAD + 2)
            nc.scalar.copy(addend[i][:], a_bank[i][:])

        def step_inner(i):
            u, t0 = STEPS[i]
            g, first, count = UNITS[u]
            inner[i] = ring.tile([P, HALF // count, count], F32, name="inner", tag="inner", align_bytes=256)
            for k in range(HALF // count):
                per_row = high_t[:, g, t0 + k : t0 + k + 1]
                nc.vector.scalar_tensor_tensor(inner[i][:, k, :], b_bank[i][:, k, :], per_row, addend[i][:, k, :], MULT, ADD)

        def step_outer(i):
            u, t0 = STEPS[i]
            g, first, count = UNITS[u]
            width = HALF // count
            if u >= LAST - 1:
                if t0 == 0:
                    slices[u] = held("outer%d" % u, [P, PACK, count], F32)
                nc.vector.tensor_tensor(slices[u][:, t0 : t0 + width, :], b_bank[i][:], inner[i][:], MULT)
                return
            outer = ring.tile([P, width, count], F32, name="outer", tag="outer", align_bytes=256)
            nc.vector.tensor_tensor(outer[:], b_bank[i][:], inner[i][:], MULT)
            if t0 == 0:
                slices[u] = held("slices%d" % u, [P, PACK, count], BF16)
            for k in range(width):
                t = t0 + k
                if (u, t) in LOW_ON_GPSIMD:
                    nc.gpsimd.tensor_scalar(slices[u][:, t, :], outer[:, k, :], 1.0, low_t[:, g, t : t + 1], MULT, ADD)
                else:
                    nc.scalar.activation(slices[u][:, t, :], outer[:, k, :], IDENT, bias=low_t[:, g, t : t + 1])

        def interleave(u):
            g, first, count = UNITS[u]
            woven[u] = held("woven", [P, PACK * count], BF16, tag={2: "woven1", 3: "woven1", 0: "tab_s", 4: "slices3"}.get(u, "woven%d" % u))
            if u >= LAST - 1:
                nc.vector.tensor_tensor(
                    woven[u][:].rearrange("p (c e t) -> p c t e", e=4, t=PACK),
                    slices[u][:].rearrange("p t (c e) -> p c t e", e=4),
                    low_t[:, g, :].unsqueeze(1).unsqueeze(3).to_broadcast([P, count // 4, PACK, 4]), ADD,
                )
            else:
                nc.gpsimd.tensor_scalar(
                    woven[u][:].rearrange("p (c t) -> p c t", t=PACK), slices[u][:].rearrange("p t c -> p c t"), 1.0, 0.0, MULT, ADD
                )

        def quantise_h(u):
            count = UNITS[u][2]
            h_c[u] = held("h_c%d" % u, [P, count], U32, tag={0: "addend8"}.get(u))
            h_s[u] = held("h_s%d" % u, [P, count], U8)
            nc.vector.quantize_mx(out=h_c[u][:].bitcast(FP8X4), scales=h_s[u][:], in_=woven[u][:])

        def unit_out(u, half, banks):
            first, count = UNITS[u][1:]
            base = GROUP0_UNIT[first]
            tokens = slice(first - UNITS[base][1], first - UNITS[base][1] + count)
            per = HALF // count
            acc = bank(banks[half % 2], [P, per, count])
            res = held("res%d%d" % (u, half), [P, per, count], F32)
            for e in range(per):
                product_out(acc[:, e, :], 0, per * half + e, h_c[base][:, tokens], h_s[base][:, tokens], e == 0, False)
            for e in range(per):
                product_out(acc[:, e, :], 1, per * half + e, h_c[u][:], h_s[u][:], False, e == per - 1)
            if u == LAST and half == 0:
                per_tile = bias_t[:, per * half : per * (half + 1)].unsqueeze(2).to_broadcast([P, per, count])
                nc.vector.tensor_tensor(res[:], acc[:], per_tile, ADD)
            else:
                for e in range(per):
                    c = per * half + e
                    nc.scalar.activation(res[:, e, :], acc[:, e, :], IDENT, bias=bias_t[:, c : c + 1])
            rows = out[per * P * half : per * P * (half + 1), first : first + count]
            nc.sync.dma_start(rows.rearrange("(c p) j -> p c j", p=P), res[:])

        for i in range(A_AHEAD):
            step_addend(i)
            if i < AHEAD:
                step_products(i)
        round_w1(1, 1, 2)
        step_inner(0)
        for i in range(len(STEPS)):
            if i + AHEAD < len(STEPS):
                step_products(i + AHEAD)
            if i + 1 < len(STEPS):
                step_inner(i + 1)
            step_outer(i)
            if i == 2:
                quantise_w1(1, 1)
            if i == 3:
                order_w2_words(1)
                w3_w = load_w3()
            if i + A_AHEAD < len(STEPS):
                step_addend(i + A_AHEAD)
            for done in QUANTISE_AT.get(i, ()):
                quantise_h(done)
            for done in INTERLEAVE_AT.get(i, ()):
                interleave(done)
            if i in (13, 15):
                unit_out(i // 2 - 4, 0, OUT_BANKS)
                unit_out(i // 2 - 4, 1, OUT_BANKS)

        interleave(LAST)
        quantise_h(LAST)
        unit_out(4, 0, A_BANKS)
        unit_out(4, 1, A_BANKS)
        unit_out(LAST, 0, B_BANKS[2:])
        unit_out(LAST, 1, B_BANKS[2:])
